import numpy as np
import ml_dtypes


def mxq(x, axis, fmt="e4m3"):
    dtype, down = {"e4m3": (ml_dtypes.float8_e4m3fn, 7), "e5m2": (ml_dtypes.float8_e5m2, 14)}[fmt]
    v = np.moveaxis(np.asarray(x, np.float32).astype(ml_dtypes.bfloat16).astype(np.float64), axis, -1)
    blocks = v.reshape(v.shape[:-1] + (-1, 32))
    amax = np.abs(blocks).max(-1, keepdims=True)
    byte = np.maximum(np.where(amax > 0, np.frexp(amax)[1] - 1 + 127, 0) - down, 1)
    scale = np.exp2(byte - 127.0)
    codes = (blocks / scale).astype(np.float32).astype(dtype).astype(np.float64)
    return np.moveaxis((codes * scale).reshape(v.shape), -1, axis)


WIDE = False


def mx_kscale(k):
    if not WIDE:
        return np.ones(k)
    levels = np.array([10, -10, 5, -5, 0])
    if k % 512:
        return np.exp2(np.random.permutation(np.resize(levels, k // 32))).repeat(32)
    a = np.empty((k // 512, 16))
    for p in range(k // 512):
        a[p, :8] = np.random.permutation(np.resize(levels, 8))
        for g in range(8):
            far = levels[np.abs(levels - a[p, g]) >= 10]
            a[p, g + 8] = far[np.random.randint(len(far))]
    return np.exp2(a.ravel()).repeat(32)


def f64(x):
    return np.asarray(x).astype(np.float64)


def striped(idx):
    return np.tile(idx.reshape(-1, 16).T, (8, 1)).astype(np.uint16)


def unstriped(offs):
    return offs[:16].T.reshape(-1).astype(np.int64)


def striped8(idx):
    return np.concatenate([x.reshape(-1, 16).T for x in idx]).astype(np.uint16)


def runs(offs, k):
    lists = np.stack([offs[16 * r : 16 * r + 16].T.reshape(-1) for r in range(8)]).astype(np.int64)
    return lists[np.arange(k) % 512 // 64]


def pack_weight(w):
    k, n = w.shape
    w = f64(np.asarray(w, np.float32).astype(ml_dtypes.bfloat16)).reshape(k // 32, 32, n)
    amax = np.abs(w).max(1)
    byte = np.clip(np.where(amax > 0, np.frexp(amax)[1] - 1 + 127 - 7, 1), 1, 254)
    scaled = (w * np.exp2(127.0 - byte)[:, None, :]).reshape(k, n).astype(np.float32)
    words = np.ascontiguousarray(scaled.reshape(k // 512, 128, 4, n).transpose(0, 1, 3, 2)).astype(ml_dtypes.float8_e4m3fn).view(np.uint8)
    return words, np.ascontiguousarray(byte.astype(np.uint8).reshape(k // 512, 16, n))


def unpack_weight(words, scales):
    g, p, n, _ = words.shape
    vals = np.ascontiguousarray(words).view(ml_dtypes.float8_e4m3fn).astype(np.float64) * np.repeat(np.exp2(scales.astype(np.float64) - 127.0), 8, axis=1)[..., None]
    return vals.transpose(0, 1, 3, 2).reshape(g * 512, n)


def sigmoid(v):
    return 1.0 / (1.0 + np.exp(-np.maximum(v, -700.0)))

def planes(y):
    n, m = y.shape
    v = y.astype(np.float32).astype(ml_dtypes.bfloat16).astype(np.float64).reshape(n // 32, 32, m)
    top = np.abs(v).max(1)
    byte = np.clip(np.where(top > 0, np.frexp(top)[1] - 1 + 127 - 7, 1), 1, 254)
    codes = (v * np.exp2(127.0 - byte)[:, None, :]).reshape(n, m).astype(np.float32).astype(ml_dtypes.float8_e4m3fn).view(np.uint8)
    words = codes.reshape(n // 512, 128, 4, m).transpose(0, 1, 3, 2)
    return np.ascontiguousarray(words), np.ascontiguousarray(byte.astype(np.uint8).reshape(n // 512, 16, m))


K, T, S, H, G = 512, 2048, 512, 512, 2048


def setup_inputs():
    n = np.random.standard_normal
    s = mx_kscale(K)[:, None]
    packed_xT = pack_weight(n((K, T)) * s)
    packed_w1 = pack_weight(n((K, H)) / np.sqrt(K) / s)
    packed_dT = pack_weight(n((K, G)) / s)
    return {
        "x_words": packed_xT[0],
        "x_scales": packed_xT[1],
        "w1_words": packed_w1[0],
        "w1_scales": packed_w1[1],
        "gs": (np.random.uniform(0.5, 1.5, (K, 1)) * s).astype(np.float32),
        "d_words": packed_dT[0],
        "d_scales": packed_dT[1],
        "offs": striped(np.random.permutation(T)[:S]),
        "b_x1": striped8(np.stack([np.random.permutation(S) for _ in range(8)])),
        "b_x2": striped8(np.stack([np.random.permutation(S) for _ in range(8)])),
        "b_x3": striped8(np.stack([np.random.permutation(S) for _ in range(8)])),
        "kq": striped8(np.random.randint(0, G, (8, H))),
    }


def reference(x_words, x_scales, w1_words, w1_scales, gs, d_words, d_scales, offs, b_x1, b_x2, b_x3, kq):
    d_kq = unpack_weight(d_words, d_scales)[np.arange(K)[:, None], runs(kq, K)]
    xq = unpack_weight(x_words, x_scales)[:, unstriped(offs)]
    y = unpack_weight(w1_words, w1_scales).T @ xq
    x1 = y[np.arange(H)[:, None], runs(b_x1, H)]
    x2 = y[np.arange(H)[:, None], runs(b_x2, H)]
    x3 = y[np.arange(H)[:, None], runs(b_x3, H)]
    mx = np.maximum(np.maximum(x1, x2), x3)
    md = np.maximum(np.minimum(x1, x2), np.minimum(np.maximum(x1, x2), x3))
    z = f64(gs) * ((mx - md) * sigmoid(md))
    out_0 = 0.0625 * ((d_kq.T @ mxq(z, 0, "e4m3")))
    return (out_0,) + planes(out_0)

@@ -1,0 +1,222 @@
+from contextlib import ExitStack
+
+import concourse.mybir as mybir
+
+F32 = mybir.dt.float32
+BF16 = mybir.dt.bfloat16
+I32 = mybir.dt.int32
+U32 = mybir.dt.uint32
+U16 = mybir.dt.uint16
+U8 = mybir.dt.uint8
+FP8X4 = mybir.dt.float8_e4m3fn_x4
+ALU = mybir.AluOpType
+ACT = mybir.ActivationFunctionType
+
+P = 128
+PACK = 4
+K, T, S, H, G = 512, 2048, 512, 512, 2048
+FLOPS = 2 * K * H * S + 2 * H * H * S
+OUT_SCALE = 0.0625
+SUB = 128
+CHUNKS = ((0, 256), (256, 128), (384, 128))
+
+
+def tile_picked_auction2_none_po_kernel(
+    tc, x_words, x_scales, w1_words, w1_scales, gs, d_words, d_scales, offs, b_x1, b_x2, b_x3, kq, out_0, out_1, out_2
+):
+    nc = tc.nc
+
+    def words_of(dram):
+        return dram[0].rearrange("p n t -> p (n t)").bitcast(I32)
+
+    with ExitStack() as ctx:
+        keep = ctx.enter_context(tc.tile_pool(name="keep", bufs=1))
+        psum = ctx.enter_context(tc.psum_pool(name="psum", bufs=1))
+
+        offs_sb = keep.tile([P, S // 16], U16, name="offs_sb")
+        b1_sb = keep.tile([P, S // 16], U16, name="b1_sb")
+        b2_sb = keep.tile([P, S // 16], U16, name="b2_sb")
+        b3_sb = keep.tile([P, S // 16], U16, name="b3_sb")
+        kq_sb = keep.tile([P, H // 16], U16, name="kq_sb")
+
+        xw_win = keep.tile([P, T], U32, name="xw_win", tag="word_table", align_bytes=64)
+        xs_win = keep.tile([P, T], U8, name="xs_win", align_bytes=64)
+        ds_win = keep.tile([P, G], U8, name="ds_win", align_bytes=64)
+        w1w_raw = keep.tile([P, H], U32, name="w1w_raw", align_bytes=64)
+        w1s_raw = keep.tile([P, H], U8, name="w1s_raw", align_bytes=64)
+        w1w = keep.tile([P, H], U32, name="w1w", align_bytes=64)
+        w1s = keep.tile([P, H], U8, name="w1s", align_bytes=64)
+        xw = keep.tile([P, S], U32, name="xw", align_bytes=64)
+        xs = keep.tile([P, S], U8, name="xs", align_bytes=64)
+        dw_pick = keep.tile([P, H], U32, name="dw_pick", align_bytes=64)
+        ds_pick = keep.tile([P, H], U8, name="ds_pick", align_bytes=64)
+        dw = keep.tile([P, H], U32, name="dw", align_bytes=64)
+        ds_dealt = keep.tile([P, H], U8, name="ds_dealt", align_bytes=64)
+        ds = keep.tile([P, H], U8, name="ds", align_bytes=64)
+        gs_sb = keep.tile([P, PACK], F32, name="gs_sb")
+        out_scales = keep.tile([P, S], U8, name="out_scales", align_bytes=64)
+
+        def deal(dst, src):
+            nc.vector.tensor_copy(out=dst.rearrange("p (t m) -> p m t", t=PACK), in_=src.rearrange("p (m t) -> p m t", t=PACK))
+
+        nc.vector.memset(xs_win[:].bitcast(I32), 0)
+        nc.vector.memset(w1s_raw[:].bitcast(I32), 0)
+        nc.vector.memset(ds_win[:].bitcast(I32), 0)
+        nc.vector.memset(ds[:].bitcast(I32), 0)
+
+        nc.sync.dma_start(offs_sb[:], offs)
+        nc.sync.dma_start(b2_sb[:], b_x2)
+        nc.sync.dma_start(b1_sb[:], b_x1)
+        nc.sync.dma_start(b3_sb[:], b_x3)
+        nc.sync.dma_start(kq_sb[:], kq)
+        nc.sync.dma_start(out=xw_win[:].bitcast(I32), in_=words_of(x_words))
+        nc.sync.dma_start(out=w1w_raw[:].bitcast(I32), in_=words_of(w1_words))
+        for r in range(4):
+            nc.scalar.dma_start(out=xs_win[r:P:32, :].bitcast(I32), in_=x_scales[0].bitcast(I32)[r:16:4, :])
+        for r in range(4):
+            nc.scalar.dma_start(out=w1s_raw[r:P:32, :].bitcast(I32), in_=w1_scales[0].bitcast(I32)[r:16:4, :])
+        for r in range(2):
+            nc.gpsimd.dma_start(out=ds_win[r:P:16, :].bitcast(I32), in_=d_scales[0].bitcast(I32)[r:16:2, :])
+        nc.gpsimd.dma_start(out=gs_sb[:], in_=gs.rearrange("(p t) o -> p (t o)", t=PACK))
+
+        deal(w1w[:].bitcast(I32), w1w_raw[:].bitcast(I32))
+        nc.vector.tensor_copy(out=xs[:], in_=xs_win[:].indirect(offs_sb[:]))
+        deal(w1s[:], w1s_raw[:])
+        half = S // 2
+        for h in range(2):
+            nc.vector.tensor_copy(
+                out=xw[:, h * half : (h + 1) * half], in_=xw_win[:].indirect(offs_sb[:, h * half // 16 : (h + 1) * half // 16])
+            )
+
+        dw_win = keep.tile([P, G], U32, name="dw_win", tag="word_table", align_bytes=64)
+        nc.sync.dma_start(out=dw_win[:].bitcast(I32), in_=words_of(d_words))
+
+        y = [keep.tile([P, S], F32, name="y%d" % t) for t in range(PACK)]
+        for t in range(PACK):
+            pieces = ((0, half), (half, half)) if t == 0 else ((0, S),)
+            for j0, n in pieces:
+                acc = psum.tile([P, n], F32, name="y_acc", tag="y_acc", bufs=5)
+                nc.tensor.matmul_mx(
+                    out=acc[:],
+                    lhsT=w1w[:, t * P : (t + 1) * P].bitcast(FP8X4),
+                    lhsT_scale=w1s[:, t * P : (t + 1) * P],
+                    rhs=xw[:, j0 : j0 + n].bitcast(FP8X4),
+                    rhs_scale=xs[:, j0 : j0 + n],
+                    start=True,
+                    stop=True,
+                )
+                nc.scalar.copy(out=y[t][:, j0 : j0 + n], in_=acc[:])
+
+        def pick_dictionary():
+            nc.vector.tensor_copy(out=ds_pick[:], in_=ds_win[:].indirect(kq_sb[:]))
+            nc.vector.tensor_copy(out=dw_pick[:], in_=dw_win[:].indirect(kq_sb[:]))
+            deal(ds_dealt[:], ds_pick[:])
+            deal(dw[:].bitcast(I32), dw_pick[:].bitcast(I32))
+            for r in range(4):
+                src = 16 * (r // 2) + r % 2
+                nc.sync.dma_start(out=ds[r:P:32, :].bitcast(I32), in_=ds_dealt[src:P:32, :].bitcast(I32))
+
+        st = {}
+
+        def planes(name, c, dtype):
+            st[name, c] = keep.tile([P, PACK, CHUNKS[c][1]], dtype, name="%s%d" % (name, c), align_bytes=64)
+            return st[name, c]
+
+        def cols(lst, c):
+            j0, n = CHUNKS[c]
+            return lst[:, j0 // 16 : (j0 + n) // 16]
+
+        def flat(tile, u):
+            return tile[:, 2 * u : 2 * u + 2, :].rearrange("p t n -> p (t n)")
+
+        def bids_a(c):
+            x2, gap12, gap12_abs, top12 = (planes(nm, c, F32) for nm in ("x2", "gap12", "gap12_abs", "top12"))
+            for t in range(PACK):
+                nc.vector.tensor_copy(out=x2[:, t, :], in_=y[t][:].indirect(cols(b2_sb, c)))
+            for t in range(PACK):
+                nc.vector.tensor_tensor(out=gap12[:, t, :], in0=y[t][:].indirect(cols(b1_sb, c)), in1=x2[:, t, :], op=ALU.subtract)
+            for u in range(2):
+                nc.scalar.activation(out=flat(gap12_abs, u), in_=flat(gap12, u), func=ACT.Abs)
+                nc.vector.scalar_tensor_tensor(
+                    out=flat(top12, u), in0=flat(gap12, u), scalar=0.0, in1=flat(x2, u), op0=ALU.max, op1=ALU.add
+                )
+
+        def bids_b(c):
+            over, gain, neg_md, gain_abs, sig = (planes(nm, c, F32) for nm in ("over", "gain", "neg_md", "gain_abs", "sig"))
+            top12, gap12_abs = st["top12", c], st["gap12_abs", c]
+            for t in range(PACK):
+                nc.vector.tensor_tensor(out=over[:, t, :], in0=y[t][:].indirect(cols(b3_sb, c)), in1=top12[:, t, :], op=ALU.subtract)
+            for u in range(2):
+                nc.vector.scalar_tensor_tensor(
+                    out=flat(gain, u), in0=flat(over, u), scalar=-1.0, in1=flat(gap12_abs, u), op0=ALU.mult, op1=ALU.min
+                )
+            for u in range(2):
+                nc.vector.scalar_tensor_tensor(
+                    out=flat(neg_md, u), in0=flat(gain, u), scalar=0.0, in1=flat(top12, u), op0=ALU.max, op1=ALU.subtract
+                )
+                nc.scalar.activation(out=flat(gain_abs, u), in_=flat(gain, u), func=ACT.Abs)
+                nc.scalar.activation(out=flat(sig, u), in_=flat(neg_md, u), func=ACT.Sigmoid, scale=-1.0)
+
+        def weigh(c):
+            n = CHUNKS[c][1]
+            z = planes("z", c, BF16)
+            for t in range(PACK):
+                nc.vector.scalar_tensor_tensor(
+                    out=z[:, t, :], in0=st["gain_abs", c][:, t, :], scalar=gs_sb[:, t : t + 1], in1=st["sig", c][:, t, :],
+                    op0=ALU.mult, op1=ALU.mult,
+                )
+            st["z_il", c] = keep.tile([P, n, PACK], BF16, name="z_il%d" % c, align_bytes=64)
+            nc.scalar.copy(out=st["z_il", c][:], in_=z[:].rearrange("p t n -> p n t"))
+
+        def second_product(c):
+            j0, n = CHUNKS[c]
+            zw = keep.tile([P, n], U32, name="zw%d" % c, align_bytes=64)
+            zs = keep.tile([P, n], U8, name="zs%d" % c, align_bytes=64)
+            nc.vector.quantize_mx(out=zw[:].bitcast(FP8X4), scales=zs[:], in_=st["z_il", c][:].rearrange("p n t -> p (n t)"))
+            res = planes("res", c, F32)
+            st["res_il", c] = keep.tile([P, n, PACK], BF16, name="res_il%d" % c, align_bytes=64)
+            for s0 in range(0, n, SUB):
+                acc = psum.tile([P, PACK, SUB], F32, name="o_acc", tag="o_acc", bufs=3)
+                for t in range(PACK):
+                    nc.tensor.matmul_mx(
+                        out=acc[:, t, :],
+                        lhsT=dw[:, t * P : (t + 1) * P].bitcast(FP8X4),
+                        lhsT_scale=ds[:, t * P : (t + 1) * P],
+                        rhs=zw[:, s0 : s0 + SUB].bitcast(FP8X4),
+                        rhs_scale=zs[:, s0 : s0 + SUB],
+                        start=True,
+                        stop=True,
+                    )
+                nc.scalar.activation(
+                    out=st["res_il", c][:, s0 : s0 + SUB, :], in_=acc[:].rearrange("p t n -> p n t"), func=ACT.Copy, scale=OUT_SCALE
+                )
+                nc.scalar.activation(out=res[:, :, s0 : s0 + SUB], in_=acc[:], func=ACT.Copy, scale=OUT_SCALE)
+            nc.sync.dma_start(out=out_0.rearrange("(p t) j -> p t j", t=PACK)[:, :, j0 : j0 + n], in_=res[:])
+
+        def hand_on(c):
+            j0, n = CHUNKS[c]
+            ow = keep.tile([P, n], U32, name="ow%d" % c, align_bytes=64)
+            nc.vector.quantize_mx(
+                out=ow[:].bitcast(FP8X4), scales=out_scales[:, j0 : j0 + n], in_=st["res_il", c][:].rearrange("p n t -> p (n t)")
+            )
+            nc.sync.dma_start(out=words_of(out_1)[:, j0 : j0 + n], in_=ow[:].bitcast(I32))
+
+        bids_a(0)
+        bids_b(0)
+        pick_dictionary()
+        bids_a(1)
+        weigh(0)
+        bids_b(1)
+        second_product(0)
+        bids_a(2)
+        weigh(1)
+        hand_on(0)
+        bids_b(2)
+        second_product(1)
+        weigh(2)
+        hand_on(1)
+        second_product(2)
+        hand_on(2)
+        for q in range(4):
+            eng = nc.scalar if q % 2 else nc.sync
+            eng.dma_start(out=out_2[0].bitcast(I32)[4 * q : 4 * q + 4, :], in_=out_scales[32 * q : 32 * q + 4, :].bitcast(I32))

@@ -18,7 +18,7 @@ K, T, S, H, G = 512, 2048, 512, 512, 2048
 FLOPS = 2 * K * H * S + 2 * H * H * S
 OUT_SCALE = 0.0625
 SUB = 128
-CHUNKS = ((0, 256), (256, 128), (384, 128))
+CHUNK = 256
 
 
 def tile_picked_auction2_none_po_kernel(
@@ -40,10 +40,9 @@ def tile_picked_auction2_none_po_kernel(
         kq_sb = keep.tile([P, H // 16], U16, name="kq_sb")
 
         xw_win = keep.tile([P, T], U32, name="xw_win", tag="word_table", align_bytes=64)
-        xs_win = keep.tile([P, T], U8, name="xs_win", align_bytes=64)
-        ds_win = keep.tile([P, G], U8, name="ds_win", align_bytes=64)
+        xs_win = keep.tile([P, T], U8, name="xs_win", tag="scale_table", align_bytes=64)
         w1w_raw = keep.tile([P, H], U32, name="w1w_raw", align_bytes=64)
-        w1s_raw = keep.tile([P, H], U8, name="w1s_raw", align_bytes=64)
+        w1s_raw = keep.tile([P, H], U8, name="w1s_raw", tag="small_load", align_bytes=64)
         w1w = keep.tile([P, H], U32, name="w1w", align_bytes=64)
         w1s = keep.tile([P, H], U8, name="w1s", align_bytes=64)
         xw = keep.tile([P, S], U32, name="xw", align_bytes=64)
@@ -53,41 +52,44 @@ def tile_picked_auction2_none_po_kernel(
         dw = keep.tile([P, H], U32, name="dw", align_bytes=64)
         ds_dealt = keep.tile([P, H], U8, name="ds_dealt", align_bytes=64)
         ds = keep.tile([P, H], U8, name="ds", align_bytes=64)
-        gs_sb = keep.tile([P, PACK], F32, name="gs_sb")
         out_scales = keep.tile([P, S], U8, name="out_scales", align_bytes=64)
 
         def deal(dst, src):
             nc.vector.tensor_copy(out=dst.rearrange("p (t m) -> p m t", t=PACK), in_=src.rearrange("p (m t) -> p m t", t=PACK))
 
-        nc.vector.memset(xs_win[:].bitcast(I32), 0)
+        nc.vector.memset(xs_win[:, : T // 2].bitcast(I32), 0)
+        nc.gpsimd.memset(xs_win[:, T // 2 :].bitcast(I32), 0)
         nc.vector.memset(w1s_raw[:].bitcast(I32), 0)
-        nc.vector.memset(ds_win[:].bitcast(I32), 0)
-        nc.vector.memset(ds[:].bitcast(I32), 0)
+        nc.gpsimd.memset(ds[:].bitcast(I32), 0)
 
+        nc.sync.dma_start(out=w1w_raw[:].bitcast(I32), in_=words_of(w1_words))
         nc.sync.dma_start(offs_sb[:], offs)
+        for r in range(4):
+            nc.sync.dma_start(out=xs_win[r:P:32, :].bitcast(I32), in_=x_scales[0].bitcast(I32)[r:16:4, :])
         nc.sync.dma_start(b2_sb[:], b_x2)
+        nc.sync.dma_start(out=xw_win[:].bitcast(I32), in_=words_of(x_words))
+        for r in range(4):
+            nc.sync.dma_start(out=w1s_raw[r:P:32, :].bitcast(I32), in_=w1_scales[0].bitcast(I32)[r:16:4, :])
         nc.sync.dma_start(b1_sb[:], b_x1)
         nc.sync.dma_start(b3_sb[:], b_x3)
         nc.sync.dma_start(kq_sb[:], kq)
-        nc.sync.dma_start(out=xw_win[:].bitcast(I32), in_=words_of(x_words))
-        nc.sync.dma_start(out=w1w_raw[:].bitcast(I32), in_=words_of(w1_words))
-        for r in range(4):
-            nc.scalar.dma_start(out=xs_win[r:P:32, :].bitcast(I32), in_=x_scales[0].bitcast(I32)[r:16:4, :])
-        for r in range(4):
-            nc.scalar.dma_start(out=w1s_raw[r:P:32, :].bitcast(I32), in_=w1_scales[0].bitcast(I32)[r:16:4, :])
-        for r in range(2):
-            nc.gpsimd.dma_start(out=ds_win[r:P:16, :].bitcast(I32), in_=d_scales[0].bitcast(I32)[r:16:2, :])
-        nc.gpsimd.dma_start(out=gs_sb[:], in_=gs.rearrange("(p t) o -> p (t o)", t=PACK))
 
         deal(w1w[:].bitcast(I32), w1w_raw[:].bitcast(I32))
-        nc.vector.tensor_copy(out=xs[:], in_=xs_win[:].indirect(offs_sb[:]))
-        deal(w1s[:], w1s_raw[:])
         half = S // 2
         for h in range(2):
-            nc.vector.tensor_copy(
-                out=xw[:, h * half : (h + 1) * half], in_=xw_win[:].indirect(offs_sb[:, h * half // 16 : (h + 1) * half // 16])
-            )
+            entries = offs_sb[:, h * half // 16 : (h + 1) * half // 16]
+            nc.vector.tensor_copy(out=xs[:, h * half : (h + 1) * half], in_=xs_win[:].indirect(entries))
+            nc.vector.tensor_copy(out=xw[:, h * half : (h + 1) * half], in_=xw_win[:].indirect(entries))
+        by_row = w1s_raw[:].rearrange("p (m t) -> p m t", t=PACK)
+        nc.vector.tensor_copy(out=w1s[:, :P], in_=by_row[:, :, 0])
+        nc.vector.tensor_copy(out=w1s[:, P:].rearrange("p (t m) -> p m t", t=PACK - 1), in_=by_row[:, :, 1:])
 
+        gs_sb = keep.tile([P, PACK], F32, name="gs_sb", tag="small_load", align_bytes=64)
+        nc.sync.dma_start(out=gs_sb[:], in_=gs.rearrange("(p t) o -> p (t o)", t=PACK))
+        ds_win = keep.tile([P, G], U8, name="ds_win", tag="scale_table", align_bytes=64)
+        nc.gpsimd.memset(ds_win[:].bitcast(I32), 0)
+        for r in range(2):
+            nc.sync.dma_start(out=ds_win[r:P:16, :].bitcast(I32), in_=d_scales[0].bitcast(I32)[r:16:2, :])
         dw_win = keep.tile([P, G], U32, name="dw_win", tag="word_table", align_bytes=64)
         nc.sync.dma_start(out=dw_win[:].bitcast(I32), in_=words_of(d_words))
 
@@ -116,65 +118,66 @@ def tile_picked_auction2_none_po_kernel(
                 src = 16 * (r // 2) + r % 2
                 nc.sync.dma_start(out=ds[r:P:32, :].bitcast(I32), in_=ds_dealt[src:P:32, :].bitcast(I32))
 
-        st = {}
+        names = ("x2", "gap12", "gap12_abs", "top12", "over", "gain", "neg_md", "gain_abs", "sig", "res")
+        st = {(nm, c): keep.tile([P, PACK, CHUNK], F32, name="%s%d" % (nm, c), align_bytes=64) for nm in names for c in range(2)}
+        z = [keep.tile([P, PACK, CHUNK], BF16, name="z%d" % c, align_bytes=64) for c in range(2)]
+        out_rows = out_0.rearrange("(p t) j -> p t j", t=PACK)
 
-        def planes(name, c, dtype):
-            st[name, c] = keep.tile([P, PACK, CHUNKS[c][1]], dtype, name="%s%d" % (name, c), align_bytes=64)
-            return st[name, c]
+        def part(name, c, t0, t1, j0, j1):
+            return st[name, c][:, t0:t1, j0:j1].rearrange("p t n -> p (t n)")
 
-        def cols(lst, c):
-            j0, n = CHUNKS[c]
-            return lst[:, j0 // 16 : (j0 + n) // 16]
+        def picked(t, lst, c, j0, j1):
+            return y[t][:].indirect(lst[:, (c * CHUNK + j0) // 16 : (c * CHUNK + j1) // 16])
 
-        def flat(tile, u):
-            return tile[:, 2 * u : 2 * u + 2, :].rearrange("p t n -> p (t n)")
-
-        def bids_a(c):
-            x2, gap12, gap12_abs, top12 = (planes(nm, c, F32) for nm in ("x2", "gap12", "gap12_abs", "top12"))
+        def fetch_x2(c):
             for t in range(PACK):
-                nc.vector.tensor_copy(out=x2[:, t, :], in_=y[t][:].indirect(cols(b2_sb, c)))
+                nc.vector.tensor_copy(out=st["x2", c][:, t, :], in_=picked(t, b2_sb, c, 0, CHUNK))
+
+        def fetch_gap12(c):
             for t in range(PACK):
-                nc.vector.tensor_tensor(out=gap12[:, t, :], in0=y[t][:].indirect(cols(b1_sb, c)), in1=x2[:, t, :], op=ALU.subtract)
-            for u in range(2):
-                nc.scalar.activation(out=flat(gap12_abs, u), in_=flat(gap12, u), func=ACT.Abs)
+                nc.vector.tensor_tensor(out=st["gap12", c][:, t, :], in0=picked(t, b1_sb, c, 0, CHUNK), in1=st["x2", c][:, t, :], op=ALU.subtract)
+
+        def make_top12(c):
+            for t0 in (0, 2):
+                at = (c, t0, t0 + 2, 0, CHUNK)
+                nc.scalar.activation(out=part("gap12_abs", *at), in_=part("gap12", *at), func=ACT.Abs)
                 nc.vector.scalar_tensor_tensor(
-                    out=flat(top12, u), in0=flat(gap12, u), scalar=0.0, in1=flat(x2, u), op0=ALU.max, op1=ALU.add
+                    out=part("top12", *at), in0=part("gap12", *at), scalar=0.0, in1=part("x2", *at), op0=ALU.max, op1=ALU.add
                 )
 
-        def bids_b(c):
-            over, gain, neg_md, gain_abs, sig = (planes(nm, c, F32) for nm in ("over", "gain", "neg_md", "gain_abs", "sig"))
-            top12, gap12_abs = st["top12", c], st["gap12_abs", c]
-            for t in range(PACK):
-                nc.vector.tensor_tensor(out=over[:, t, :], in0=y[t][:].indirect(cols(b3_sb, c)), in1=top12[:, t, :], op=ALU.subtract)
-            for u in range(2):
-                nc.vector.scalar_tensor_tensor(
-                    out=flat(gain, u), in0=flat(over, u), scalar=-1.0, in1=flat(gap12_abs, u), op0=ALU.mult, op1=ALU.min
-                )
-            for u in range(2):
-                nc.vector.scalar_tensor_tensor(
-                    out=flat(neg_md, u), in0=flat(gain, u), scalar=0.0, in1=flat(top12, u), op0=ALU.max, op1=ALU.subtract
-                )
-                nc.scalar.activation(out=flat(gain_abs, u), in_=flat(gain, u), func=ACT.Abs)
-                nc.scalar.activation(out=flat(sig, u), in_=flat(neg_md, u), func=ACT.Sigmoid, scale=-1.0)
+        def fetch_over(c, t, j0=0, j1=CHUNK):
+            at = (c, t, t + 1, j0, j1)
+            nc.vector.tensor_tensor(out=part("over", *at), in0=picked(t, b3_sb, c, j0, j1), in1=part("top12", *at), op=ALU.subtract)
 
-        def weigh(c):
-            n = CHUNKS[c][1]
-            z = planes("z", c, BF16)
-            for t in range(PACK):
-                nc.vector.scalar_tensor_tensor(
-                    out=z[:, t, :], in0=st["gain_abs", c][:, t, :], scalar=gs_sb[:, t : t + 1], in1=st["sig", c][:, t, :],
-                    op0=ALU.mult, op1=ALU.mult,
-                )
-            st["z_il", c] = keep.tile([P, n, PACK], BF16, name="z_il%d" % c, align_bytes=64)
-            nc.scalar.copy(out=st["z_il", c][:], in_=z[:].rearrange("p t n -> p n t"))
+        def make_gain(*at):
+            nc.vector.scalar_tensor_tensor(
+                out=part("gain", *at), in0=part("over", *at), scalar=-1.0, in1=part("gap12_abs", *at), op0=ALU.mult, op1=ALU.min
+            )
+            nc.scalar.activation(out=part("gain_abs", *at), in_=part("gain", *at), func=ACT.Abs)
 
-        def second_product(c):
-            j0, n = CHUNKS[c]
-            zw = keep.tile([P, n], U32, name="zw%d" % c, align_bytes=64)
-            zs = keep.tile([P, n], U8, name="zs%d" % c, align_bytes=64)
-            nc.vector.quantize_mx(out=zw[:].bitcast(FP8X4), scales=zs[:], in_=st["z_il", c][:].rearrange("p n t -> p (n t)"))
-            res = planes("res", c, F32)
-            st["res_il", c] = keep.tile([P, n, PACK], BF16, name="res_il%d" % c, align_bytes=64)
+        def make_sig(*at):
+            nc.vector.scalar_tensor_tensor(
+                out=part("neg_md", *at), in0=part("gain", *at), scalar=0.0, in1=part("top12", *at), op0=ALU.max, op1=ALU.subtract
+            )
+            nc.scalar.activation(out=part("sig", *at), in_=part("neg_md", *at), func=ACT.Sigmoid, scale=-1.0)
+
+        def weigh(c, t, j0=0, j1=CHUNK):
+            at = (c, t, t + 1, j0, j1)
+            nc.vector.scalar_tensor_tensor(
+                out=z[c][:, t, j0:j1], in0=part("gain_abs", *at), scalar=gs_sb[:, t : t + 1], in1=part("sig", *at), op0=ALU.mult, op1=ALU.mult
+            )
+
+        def weave(copy, src, name):
+            woven = keep.tile([P, src.shape[2], PACK], BF16, name=name, align_bytes=64)
+            copy(out=woven[:], in_=src.rearrange("p t n -> p n t"))
+            return woven
+
+        def second_product(c, j0, j1, z_woven):
+            n = j1 - j0
+            zw = keep.tile([P, n], U32, name="zw%d_%d" % (c, j0), align_bytes=64)
+            zs = keep.tile([P, n], U8, name="zs%d_%d" % (c, j0), align_bytes=64)
+            nc.vector.quantize_mx(out=zw[:].bitcast(FP8X4), scales=zs[:], in_=z_woven[:].rearrange("p n t -> p (n t)"))
+            res = st["res", c]
             for s0 in range(0, n, SUB):
                 acc = psum.tile([P, PACK, SUB], F32, name="o_acc", tag="o_acc", bufs=3)
                 for t in range(PACK):
@@ -187,36 +190,59 @@ def tile_picked_auction2_none_po_kernel(
                         start=True,
                         stop=True,
                     )
-                nc.scalar.activation(
-                    out=st["res_il", c][:, s0 : s0 + SUB, :], in_=acc[:].rearrange("p t n -> p n t"), func=ACT.Copy, scale=OUT_SCALE
-                )
-                nc.scalar.activation(out=res[:, :, s0 : s0 + SUB], in_=acc[:], func=ACT.Copy, scale=OUT_SCALE)
-            nc.sync.dma_start(out=out_0.rearrange("(p t) j -> p t j", t=PACK)[:, :, j0 : j0 + n], in_=res[:])
+                nc.scalar.activation(out=res[:, :, j0 + s0 : j0 + s0 + SUB], in_=acc[:], func=ACT.Copy, scale=OUT_SCALE)
+            nc.sync.dma_start(out=out_rows[:, :, c * CHUNK + j0 : c * CHUNK + j1], in_=res[:, :, j0:j1])
 
-        def hand_on(c):
-            j0, n = CHUNKS[c]
-            ow = keep.tile([P, n], U32, name="ow%d" % c, align_bytes=64)
-            nc.vector.quantize_mx(
-                out=ow[:].bitcast(FP8X4), scales=out_scales[:, j0 : j0 + n], in_=st["res_il", c][:].rearrange("p n t -> p (n t)")
-            )
-            nc.sync.dma_start(out=words_of(out_1)[:, j0 : j0 + n], in_=ow[:].bitcast(I32))
+        def hand_on(c, j0, j1, res_woven):
+            cols = slice(c * CHUNK + j0, c * CHUNK + j1)
+            ow = keep.tile([P, j1 - j0], U32, name="ow%d_%d" % (c, j0), align_bytes=64)
+            nc.vector.quantize_mx(out=ow[:].bitcast(FP8X4), scales=out_scales[:, cols], in_=res_woven[:].rearrange("p n t -> p (n t)"))
+            nc.sync.dma_start(out=words_of(out_1)[:, cols], in_=ow[:].bitcast(I32))
 
-        bids_a(0)
-        bids_b(0)
+        fetch_x2(0)
+        fetch_gap12(0)
+        make_top12(0)
+        for t in range(PACK):
+            fetch_over(0, t)
+        for t0 in (0, 2):
+            make_gain(0, t0, t0 + 2, 0, CHUNK)
+        for t0 in (0, 2):
+            make_sig(0, t0, t0 + 2, 0, CHUNK)
         pick_dictionary()
-        bids_a(1)
-        weigh(0)
-        bids_b(1)
-        second_product(0)
-        bids_a(2)
-        weigh(1)
-        hand_on(0)
-        bids_b(2)
-        second_product(1)
-        weigh(2)
-        hand_on(1)
-        second_product(2)
-        hand_on(2)
+        fetch_x2(1)
+        for t in range(PACK):
+            weigh(0, t)
+        z_woven = weave(nc.scalar.copy, z[0][:], "z_woven0")
+        fetch_gap12(1)
+        second_product(0, 0, CHUNK, z_woven)
+        res_woven = weave(nc.scalar.copy, st["res", 0][:], "res_woven0")
+        make_top12(1)
+        fetch_over(1, 0)
+        fetch_over(1, 1)
+        fetch_over(1, 2)
+        make_gain(1, 0, 2, 0, CHUNK)
+        fetch_over(1, 3, 0, SUB)
+        make_sig(1, 0, 2, 0, CHUNK)
+        make_gain(1, 2, 3, 0, CHUNK)
+        fetch_over(1, 3, SUB, CHUNK)
+        make_sig(1, 2, 3, 0, CHUNK)
+        make_gain(1, 3, 4, 0, SUB)
+        make_gain(1, 3, 4, SUB, CHUNK)
+        make_sig(1, 3, 4, 0, SUB)
+        make_sig(1, 3, 4, SUB, CHUNK)
+        hand_on(0, 0, CHUNK, res_woven)
+        for t in range(3):
+            weigh(1, t)
+        weigh(1, 3, 0, SUB)
+        z_woven_a = weave(nc.scalar.copy, z[1][:, :, 0:SUB], "z_woven1a")
+        weigh(1, 3, SUB, CHUNK)
+        z_woven_b = weave(nc.vector.tensor_copy, z[1][:, :, SUB:CHUNK], "z_woven1b")
+        second_product(1, 0, SUB, z_woven_a)
+        second_product(1, SUB, CHUNK, z_woven_b)
+        res_woven_a = weave(nc.vector.tensor_copy, st["res", 1][:, :, 0:SUB], "res_woven1a")
+        hand_on(1, 0, SUB, res_woven_a)
+        res_woven_b = weave(nc.vector.tensor_copy, st["res", 1][:, :, SUB:CHUNK], "res_woven1b")
+        hand_on(1, SUB, CHUNK, res_woven_b)
         for q in range(4):
             eng = nc.scalar if q % 2 else nc.sync
             eng.dma_start(out=out_2[0].bitcast(I32)[4 * q : 4 * q + 4, :], in_=out_scales[32 * q : 32 * q + 4, :].bitcast(I32))

@@ -1,6 +1,7 @@
 from contextlib import ExitStack
 
 import concourse.mybir as mybir
+from concourse.masks import make_identity
 
 F32 = mybir.dt.float32
 BF16 = mybir.dt.bfloat16
@@ -18,7 +19,9 @@ K, T, S, H, G = 512, 2048, 512, 512, 2048
 FLOPS = 2 * K * H * S + 2 * H * H * S
 OUT_SCALE = 0.0625
 SUB = 128
+UNITS = (((0, 1), 0), ((2, 3), 0), ((0, 1), 256), ((2, 3), 256))
 CHUNK = 256
+WIDTH = 512
 
 
 def tile_picked_auction2_none_po_kernel(
@@ -39,210 +42,298 @@ def tile_picked_auction2_none_po_kernel(
         b3_sb = keep.tile([P, S // 16], U16, name="b3_sb")
         kq_sb = keep.tile([P, H // 16], U16, name="kq_sb")
 
-        xw_win = keep.tile([P, T], U32, name="xw_win", tag="word_table", align_bytes=64)
-        xs_win = keep.tile([P, T], U8, name="xs_win", tag="scale_table", align_bytes=64)
+        xw_win = keep.tile([P, T], U32, name="xw_win", align_bytes=64)
+        dw_win = keep.tile([P, G], U32, name="dw_win", align_bytes=64)
+        xs_win = keep.tile([P, T], U8, name="xs_win", align_bytes=64)
+        ds_win = keep.tile([P, G], U8, name="ds_win", align_bytes=64)
         w1w_raw = keep.tile([P, H], U32, name="w1w_raw", align_bytes=64)
-        w1s_raw = keep.tile([P, H], U8, name="w1s_raw", tag="small_load", align_bytes=64)
+        w1s_raw = keep.tile([P, H], U8, name="w1s_raw", tag="scales_to_deal", align_bytes=64)
         w1w = keep.tile([P, H], U32, name="w1w", align_bytes=64)
         w1s = keep.tile([P, H], U8, name="w1s", align_bytes=64)
         xw = keep.tile([P, S], U32, name="xw", align_bytes=64)
         xs = keep.tile([P, S], U8, name="xs", align_bytes=64)
-        dw_pick = keep.tile([P, H], U32, name="dw_pick", align_bytes=64)
         ds_pick = keep.tile([P, H], U8, name="ds_pick", align_bytes=64)
         dw = keep.tile([P, H], U32, name="dw", align_bytes=64)
-        ds_dealt = keep.tile([P, H], U8, name="ds_dealt", align_bytes=64)
         ds = keep.tile([P, H], U8, name="ds", align_bytes=64)
         out_scales = keep.tile([P, S], U8, name="out_scales", align_bytes=64)
+        gs_sb = keep.tile([P, PACK], F32, name="gs_sb")
+        gs2 = keep.tile([P, PACK], F32, name="gs2")
 
         def deal(dst, src):
             nc.vector.tensor_copy(out=dst.rearrange("p (t m) -> p m t", t=PACK), in_=src.rearrange("p (m t) -> p m t", t=PACK))
 
-        nc.vector.memset(xs_win[:, : T // 2].bitcast(I32), 0)
-        nc.gpsimd.memset(xs_win[:, T // 2 :].bitcast(I32), 0)
-        nc.vector.memset(w1s_raw[:].bitcast(I32), 0)
-        nc.gpsimd.memset(ds[:].bitcast(I32), 0)
+        def bank(i, shape, name):
+            return psum.tile(shape, F32, name=name, tag="bank%d" % i)
 
-        nc.sync.dma_start(out=w1w_raw[:].bitcast(I32), in_=words_of(w1_words))
+        warm_in = keep.tile([P, 1], F32, name="warm_in")
+        warm_out = keep.tile([P, 1], F32, name="warm_out")
+        nc.vector.memset(warm_in[:], 0.0)
+        nc.scalar.activation(out=warm_out[:], in_=warm_in[:], func=ACT.Sigmoid)
+        nc.vector.memset(ds_win[:].bitcast(I32), 0)
+        for plane in (xs_win, w1s_raw, ds):
+            nc.gpsimd.memset(plane[:].bitcast(I32), 0)
+        ident = keep.tile([P, P], F32, name="ident", align_bytes=64)
+        make_identity(nc, ident[:])
+
         nc.sync.dma_start(offs_sb[:], offs)
+        nc.sync.dma_start(kq_sb[:], kq)
         for r in range(4):
             nc.sync.dma_start(out=xs_win[r:P:32, :].bitcast(I32), in_=x_scales[0].bitcast(I32)[r:16:4, :])
-        nc.sync.dma_start(b2_sb[:], b_x2)
+        nc.sync.dma_start(out=ds_win[0:P:8, :].bitcast(I32), in_=d_scales[0].bitcast(I32))
         nc.sync.dma_start(out=xw_win[:].bitcast(I32), in_=words_of(x_words))
+        nc.sync.dma_start(out=w1w_raw[:].bitcast(I32), in_=words_of(w1_words))
         for r in range(4):
             nc.sync.dma_start(out=w1s_raw[r:P:32, :].bitcast(I32), in_=w1_scales[0].bitcast(I32)[r:16:4, :])
+        nc.sync.dma_start(out=dw_win[:].bitcast(I32), in_=words_of(d_words))
+        nc.sync.dma_start(b2_sb[:], b_x2)
         nc.sync.dma_start(b1_sb[:], b_x1)
         nc.sync.dma_start(b3_sb[:], b_x3)
-        nc.sync.dma_start(kq_sb[:], kq)
-
-        deal(w1w[:].bitcast(I32), w1w_raw[:].bitcast(I32))
-        half = S // 2
-        for h in range(2):
-            entries = offs_sb[:, h * half // 16 : (h + 1) * half // 16]
-            nc.vector.tensor_copy(out=xs[:, h * half : (h + 1) * half], in_=xs_win[:].indirect(entries))
-            nc.vector.tensor_copy(out=xw[:, h * half : (h + 1) * half], in_=xw_win[:].indirect(entries))
-        by_row = w1s_raw[:].rearrange("p (m t) -> p m t", t=PACK)
-        nc.vector.tensor_copy(out=w1s[:, :P], in_=by_row[:, :, 0])
-        nc.vector.tensor_copy(out=w1s[:, P:].rearrange("p (t m) -> p m t", t=PACK - 1), in_=by_row[:, :, 1:])
-
-        gs_sb = keep.tile([P, PACK], F32, name="gs_sb", tag="small_load", align_bytes=64)
         nc.sync.dma_start(out=gs_sb[:], in_=gs.rearrange("(p t) o -> p (t o)", t=PACK))
-        ds_win = keep.tile([P, G], U8, name="ds_win", tag="scale_table", align_bytes=64)
-        nc.gpsimd.memset(ds_win[:].bitcast(I32), 0)
-        for r in range(2):
-            nc.sync.dma_start(out=ds_win[r:P:16, :].bitcast(I32), in_=d_scales[0].bitcast(I32)[r:16:2, :])
-        dw_win = keep.tile([P, G], U32, name="dw_win", tag="word_table", align_bytes=64)
-        nc.sync.dma_start(out=dw_win[:].bitcast(I32), in_=words_of(d_words))
 
-        y = [keep.tile([P, S], F32, name="y%d" % t) for t in range(PACK)]
-        for t in range(PACK):
-            pieces = ((0, half), (half, half)) if t == 0 else ((0, S),)
-            for j0, n in pieces:
-                acc = psum.tile([P, n], F32, name="y_acc", tag="y_acc", bufs=5)
-                nc.tensor.matmul_mx(
-                    out=acc[:],
-                    lhsT=w1w[:, t * P : (t + 1) * P].bitcast(FP8X4),
-                    lhsT_scale=w1s[:, t * P : (t + 1) * P],
-                    rhs=xw[:, j0 : j0 + n].bitcast(FP8X4),
-                    rhs_scale=xs[:, j0 : j0 + n],
-                    start=True,
-                    stop=True,
-                )
-                nc.scalar.copy(out=y[t][:, j0 : j0 + n], in_=acc[:])
+        half = S // 2
+        w1_moves = ((w1w[:].bitcast(I32), w1w_raw[:].bitcast(I32)), (w1s[:], w1s_raw[:]))
+        nc.vector.tensor_copy(out=xs[:], in_=xs_win[:].indirect(offs_sb[:]))
+        nc.vector.tensor_copy(out=ds_pick[:], in_=ds_win[:].indirect(kq_sb[:]))
+        for h in range(2):
+            nc.vector.tensor_copy(out=xw[:, h * half : (h + 1) * half], in_=xw_win[:].indirect(offs_sb[:, h * half // 16 : (h + 1) * half // 16]))
+        for dst, src in w1_moves:
+            nc.vector.tensor_copy(out=dst[:, :P], in_=src.rearrange("p (m t) -> p m t", t=PACK)[:, :, 0])
+        for dst, src in w1_moves:
+            nc.vector.tensor_copy(
+                out=dst[:, P:].rearrange("p (t m) -> p m t", t=PACK - 1), in_=src.rearrange("p (m t) -> p m t", t=PACK)[:, :, 1:]
+            )
+        ds_dealt = keep.tile([P, H], U8, name="ds_dealt", tag="scales_to_deal", align_bytes=64)
+        deal(ds_dealt[:], ds_pick[:])
+        for r in range(4):
+            nc.sync.dma_start(out=ds[r:P:32, :].bitcast(I32), in_=ds_dealt[8 * r : P : 32, :].bitcast(I32))
 
-        def pick_dictionary():
-            nc.vector.tensor_copy(out=ds_pick[:], in_=ds_win[:].indirect(kq_sb[:]))
-            nc.vector.tensor_copy(out=dw_pick[:], in_=dw_win[:].indirect(kq_sb[:]))
-            deal(ds_dealt[:], ds_pick[:])
-            deal(dw[:].bitcast(I32), dw_pick[:].bitcast(I32))
-            for r in range(4):
-                src = 16 * (r // 2) + r % 2
-                nc.sync.dma_start(out=ds[r:P:32, :].bitcast(I32), in_=ds_dealt[src:P:32, :].bitcast(I32))
+        neg_y = [keep.tile([P, S], F32, name="neg_y%d" % t) for t in range(PACK)]
+        for b, (t, j0, n) in enumerate(((0, 0, half), (0, half, half), (1, 0, S), (2, 0, S), (3, 0, S))):
+            acc = bank(b, [P, n], "y_acc")
+            nc.tensor.matmul_mx(
+                out=acc[:],
+                lhsT=w1w[:, t * P : (t + 1) * P].bitcast(FP8X4),
+                lhsT_scale=w1s[:, t * P : (t + 1) * P],
+                rhs=xw[:, j0 : j0 + n].bitcast(FP8X4),
+                rhs_scale=xs[:, j0 : j0 + n],
+                start=True,
+                stop=True,
+            )
+            nc.scalar.activation(out=neg_y[t][:, j0 : j0 + n], in_=acc[:], func=ACT.Copy, scale=-1.0)
+        nc.scalar.activation(out=gs2[:], in_=gs_sb[:], func=ACT.Copy, scale=2.0)
 
-        names = ("x2", "gap12", "gap12_abs", "top12", "over", "gain", "neg_md", "gain_abs", "sig", "res")
-        st = {(nm, c): keep.tile([P, PACK, CHUNK], F32, name="%s%d" % (nm, c), align_bytes=64) for nm in names for c in range(2)}
+        st = {}
         z = [keep.tile([P, PACK, CHUNK], BF16, name="z%d" % c, align_bytes=64) for c in range(2)]
         out_rows = out_0.rearrange("(p t) j -> p t j", t=PACK)
 
-        def part(name, c, t0, t1, j0, j1):
-            return st[name, c][:, t0:t1, j0:j1].rearrange("p t n -> p (t n)")
+        def new(name, u, tag=None):
+            st[name, u] = keep.tile([P, 2, CHUNK], F32, name="%s%d" % (name, u), tag=tag or "%s%d" % (name, u), align_bytes=64)
+            return st[name, u]
 
-        def picked(t, lst, c, j0, j1):
-            return y[t][:].indirect(lst[:, (c * CHUNK + j0) // 16 : (c * CHUNK + j1) // 16])
+        def new_rows(name, u, tag=None):
+            st[name, u] = [
+                keep.tile([P, CHUNK], F32, name="%s%d_%d" % (name, u, e), tag="%s_%d" % (tag or "%s%d" % (name, u), e), align_bytes=64)
+                for e in range(2)
+            ]
 
-        def fetch_x2(c):
-            for t in range(PACK):
-                nc.vector.tensor_copy(out=st["x2", c][:, t, :], in_=picked(t, b2_sb, c, 0, CHUNK))
+        def part(name, u, e, c0=0, c1=CHUNK):
+            held = st[name, u]
+            return held[e][:, c0:c1] if isinstance(held, list) else held[:, e, c0:c1]
 
-        def fetch_gap12(c):
-            for t in range(PACK):
-                nc.vector.tensor_tensor(out=st["gap12", c][:, t, :], in0=picked(t, b1_sb, c, 0, CHUNK), in1=st["x2", c][:, t, :], op=ALU.subtract)
+        def picked(lst, u, e, c0=0, c1=CHUNK):
+            ts, j0 = UNITS[u]
+            return neg_y[ts[e]][:].indirect(lst[:, (j0 + c0) // 16 : (j0 + c1) // 16])
 
-        def make_top12(c):
-            for t0 in (0, 2):
-                at = (c, t0, t0 + 2, 0, CHUNK)
-                nc.scalar.activation(out=part("gap12_abs", *at), in_=part("gap12", *at), func=ACT.Abs)
+        def fetch_n2(u, tag=None):
+            new_rows("n2", u, tag)
+            for e in range(2):
+                nc.vector.tensor_copy(out=part("n2", u, e), in_=picked(b2_sb, u, e))
+
+        def fetch_gap(u, factor, tag=None, abs_tag=None):
+            gap, gap_abs = new("gap", u, tag), new("gap_abs", u, abs_tag)
+            for e in range(2):
+                nc.vector.tensor_tensor(out=gap[:, e, :], in0=picked(b1_sb, u, e), in1=part("n2", u, e), op=ALU.subtract)
+            nc.scalar.activation(out=gap_abs[:], in_=gap[:], func=ACT.Abs, scale=factor)
+
+        def make_low(u, tag=None):
+            low = new("low", u, tag)
+            for e in range(2):
                 nc.vector.scalar_tensor_tensor(
-                    out=part("top12", *at), in0=part("gap12", *at), scalar=0.0, in1=part("x2", *at), op0=ALU.max, op1=ALU.add
+                    out=low[:, e, :], in0=st["gap", u][:, e, :], scalar=0.0, in1=part("n2", u, e), op0=ALU.min, op1=ALU.add
                 )
 
-        def fetch_over(c, t, j0=0, j1=CHUNK):
-            at = (c, t, t + 1, j0, j1)
-            nc.vector.tensor_tensor(out=part("over", *at), in0=picked(t, b3_sb, c, j0, j1), in1=part("top12", *at), op=ALU.subtract)
-
-        def make_gain(*at):
-            nc.vector.scalar_tensor_tensor(
-                out=part("gain", *at), in0=part("over", *at), scalar=-1.0, in1=part("gap12_abs", *at), op0=ALU.mult, op1=ALU.min
-            )
-            nc.scalar.activation(out=part("gain_abs", *at), in_=part("gain", *at), func=ACT.Abs)
-
-        def make_sig(*at):
-            nc.vector.scalar_tensor_tensor(
-                out=part("neg_md", *at), in0=part("gain", *at), scalar=0.0, in1=part("top12", *at), op0=ALU.max, op1=ALU.subtract
-            )
-            nc.scalar.activation(out=part("sig", *at), in_=part("neg_md", *at), func=ACT.Sigmoid, scale=-1.0)
-
-        def weigh(c, t, j0=0, j1=CHUNK):
-            at = (c, t, t + 1, j0, j1)
-            nc.vector.scalar_tensor_tensor(
-                out=z[c][:, t, j0:j1], in0=part("gain_abs", *at), scalar=gs_sb[:, t : t + 1], in1=part("sig", *at), op0=ALU.mult, op1=ALU.mult
+        def fetch_over(u, e, c0=0, c1=CHUNK):
+            nc.vector.tensor_tensor(
+                out=part("over", u, e, c0, c1), in0=picked(b3_sb, u, e, c0, c1), in1=st["low", u][:, e, c0:c1], op=ALU.subtract
             )
 
-        def weave(copy, src, name):
-            woven = keep.tile([P, src.shape[2], PACK], BF16, name=name, align_bytes=64)
+        def make_gain(u, factor, at):
+            nc.vector.scalar_tensor_tensor(
+                out=st["gain", u][at], in0=st["over", u][at], scalar=factor, in1=st["gap_abs", u][at], op0=ALU.mult, op1=ALU.min
+            )
+            nc.scalar.activation(out=st["gain_abs", u][at], in_=st["gain", u][at], func=ACT.Abs)
+
+        def sig_by_transposes(u, banks):
+            sig_turned = keep.tile([P, 2, CHUNK], F32, name="sig_turned%d" % u, tag="sig_turned%d" % u, align_bytes=64)
+            for e in range(2):
+                turned = bank(banks[e], [P, CHUNK], "turned")
+                for c0 in range(0, CHUNK, P):
+                    for i, name in enumerate(("low", "gain", "gain_abs")):
+                        nc.tensor.matmul(
+                            out=turned[:, c0 : c0 + P], lhsT=part(name, u, e, c0, c0 + P), rhs=ident[:], is_transpose=True, start=i == 0, stop=i == 2
+                        )
+                nc.scalar.activation(out=sig_turned[:, e, :], in_=turned[:], func=ACT.Sigmoid, scale=-1.0)
+            st["sig", u] = [bank(banks[2 + e], [P, CHUNK], "sig") for e in range(2)]
+            for e in range(2):
+                for c0 in range(0, CHUNK, P):
+                    nc.tensor.transpose(part("sig", u, e, c0, c0 + P), sig_turned[:, e, c0 : c0 + P], ident[:])
+
+        def sig_direct(u, at):
+            nc.vector.scalar_tensor_tensor(
+                out=st["neg_md", u][at], in0=st["gain", u][at], scalar=0.0, in1=st["low", u][at], op0=ALU.max, op1=ALU.add
+            )
+            nc.scalar.activation(out=st["sig", u][at], in_=st["neg_md", u][at], func=ACT.Sigmoid, scale=-1.0)
+
+        def weigh(u, weight, c0=0, c1=CHUNK):
+            ts, j0 = UNITS[u]
+            for e, t in enumerate(ts):
+                nc.vector.scalar_tensor_tensor(
+                    out=z[j0 // CHUNK][:, t, c0:c1], in0=part("gain_abs", u, e, c0, c1), scalar=weight[:, t : t + 1],
+                    in1=part("sig", u, e, c0, c1), op0=ALU.mult, op1=ALU.mult,
+                )
+
+        def weave(copy, src, name, tag=None):
+            woven = keep.tile([P, src.shape[2], PACK], BF16, name=name, tag=tag or name, align_bytes=64)
             copy(out=woven[:], in_=src.rearrange("p t n -> p n t"))
             return woven
 
-        def second_product(c, j0, j1, z_woven):
-            n = j1 - j0
-            zw = keep.tile([P, n], U32, name="zw%d_%d" % (c, j0), align_bytes=64)
-            zs = keep.tile([P, n], U8, name="zs%d_%d" % (c, j0), align_bytes=64)
+        def quantise_z(j0, n, z_woven):
+            zw = keep.tile([P, n], U32, name="zw%d" % j0, align_bytes=64)
+            zs = keep.tile([P, n], U8, name="zs%d" % j0, align_bytes=64)
             nc.vector.quantize_mx(out=zw[:].bitcast(FP8X4), scales=zs[:], in_=z_woven[:].rearrange("p n t -> p (n t)"))
-            res = st["res", c]
-            for s0 in range(0, n, SUB):
-                acc = psum.tile([P, PACK, SUB], F32, name="o_acc", tag="o_acc", bufs=3)
+            return zw, zs
+
+        def product(out, t, zw, zs):
+            nc.tensor.matmul_mx(
+                out=out,
+                lhsT=dw[:, t * P : (t + 1) * P].bitcast(FP8X4),
+                lhsT_scale=ds[:, t * P : (t + 1) * P],
+                rhs=zw.bitcast(FP8X4),
+                rhs_scale=zs,
+                start=True,
+                stop=True,
+            )
+
+        def second_product(j0, n, zq, banks):
+            zw, zs = zq
+            res_woven = keep.tile([P, n, PACK], BF16, name="res_woven%d" % j0, align_bytes=64)
+            accs = []
+            for s0, b in zip(range(0, n, SUB), banks):
+                acc = bank(b, [P, PACK, SUB], "o_acc")
                 for t in range(PACK):
-                    nc.tensor.matmul_mx(
-                        out=acc[:, t, :],
-                        lhsT=dw[:, t * P : (t + 1) * P].bitcast(FP8X4),
-                        lhsT_scale=ds[:, t * P : (t + 1) * P],
-                        rhs=zw[:, s0 : s0 + SUB].bitcast(FP8X4),
-                        rhs_scale=zs[:, s0 : s0 + SUB],
-                        start=True,
-                        stop=True,
-                    )
-                nc.scalar.activation(out=res[:, :, j0 + s0 : j0 + s0 + SUB], in_=acc[:], func=ACT.Copy, scale=OUT_SCALE)
-            nc.sync.dma_start(out=out_rows[:, :, c * CHUNK + j0 : c * CHUNK + j1], in_=res[:, :, j0:j1])
+                    product(acc[:, t, :], t, zw[:, s0 : s0 + SUB], zs[:, s0 : s0 + SUB])
+                nc.scalar.activation(
+                    out=res_woven[:, s0 : s0 + SUB, :], in_=acc[:].rearrange("p t n -> p n t"), func=ACT.Copy, scale=OUT_SCALE
+                )
+                accs.append(acc)
+            return res_woven, accs
 
-        def hand_on(c, j0, j1, res_woven):
-            cols = slice(c * CHUNK + j0, c * CHUNK + j1)
-            ow = keep.tile([P, j1 - j0], U32, name="ow%d_%d" % (c, j0), align_bytes=64)
-            nc.vector.quantize_mx(out=ow[:].bitcast(FP8X4), scales=out_scales[:, cols], in_=res_woven[:].rearrange("p n t -> p (n t)"))
-            nc.sync.dma_start(out=words_of(out_1)[:, cols], in_=ow[:].bitcast(I32))
+        def store_result(j0, accs, tag):
+            res = keep.tile([P, PACK, SUB * len(accs)], F32, name="res%d" % j0, tag=tag, align_bytes=64)
+            for i, acc in enumerate(accs):
+                nc.scalar.activation(out=res[:, :, i * SUB : (i + 1) * SUB], in_=acc[:], func=ACT.Copy, scale=OUT_SCALE)
+            nc.sync.dma_start(out=out_rows[:, :, j0 : j0 + SUB * len(accs)], in_=res[:])
 
-        fetch_x2(0)
-        fetch_gap12(0)
-        make_top12(0)
-        for t in range(PACK):
-            fetch_over(0, t)
-        for t0 in (0, 2):
-            make_gain(0, t0, t0 + 2, 0, CHUNK)
-        for t0 in (0, 2):
-            make_sig(0, t0, t0 + 2, 0, CHUNK)
-        pick_dictionary()
-        fetch_x2(1)
-        for t in range(PACK):
-            weigh(0, t)
-        z_woven = weave(nc.scalar.copy, z[0][:], "z_woven0")
-        fetch_gap12(1)
-        second_product(0, 0, CHUNK, z_woven)
-        res_woven = weave(nc.scalar.copy, st["res", 0][:], "res_woven0")
-        make_top12(1)
-        fetch_over(1, 0)
-        fetch_over(1, 1)
-        fetch_over(1, 2)
-        make_gain(1, 0, 2, 0, CHUNK)
-        fetch_over(1, 3, 0, SUB)
-        make_sig(1, 0, 2, 0, CHUNK)
-        make_gain(1, 2, 3, 0, CHUNK)
-        fetch_over(1, 3, SUB, CHUNK)
-        make_sig(1, 2, 3, 0, CHUNK)
-        make_gain(1, 3, 4, 0, SUB)
-        make_gain(1, 3, 4, SUB, CHUNK)
-        make_sig(1, 3, 4, 0, SUB)
-        make_sig(1, 3, 4, SUB, CHUNK)
-        hand_on(0, 0, CHUNK, res_woven)
-        for t in range(3):
-            weigh(1, t)
-        weigh(1, 3, 0, SUB)
-        z_woven_a = weave(nc.scalar.copy, z[1][:, :, 0:SUB], "z_woven1a")
-        weigh(1, 3, SUB, CHUNK)
-        z_woven_b = weave(nc.vector.tensor_copy, z[1][:, :, SUB:CHUNK], "z_woven1b")
-        second_product(1, 0, SUB, z_woven_a)
-        second_product(1, SUB, CHUNK, z_woven_b)
-        res_woven_a = weave(nc.vector.tensor_copy, st["res", 1][:, :, 0:SUB], "res_woven1a")
-        hand_on(1, 0, SUB, res_woven_a)
-        res_woven_b = weave(nc.vector.tensor_copy, st["res", 1][:, :, SUB:CHUNK], "res_woven1b")
-        hand_on(1, SUB, CHUNK, res_woven_b)
+        def last_product(j0, n, zq, banks, queue):
+            zw, zs = zq
+            res = keep.tile([P, PACK, n], F32, name="res%d" % j0, align_bytes=64)
+            for i, b in enumerate(banks):
+                acc = bank(b, [P, 2, n], "o_acc")
+                for e in range(2):
+                    product(acc[:, e, :], 2 * i + e, zw[:], zs[:])
+                if i == 0:
+                    nc.scalar.activation(out=res[:, 0:2, :], in_=acc[:], func=ACT.Copy, scale=OUT_SCALE)
+                else:
+                    nc.vector.tensor_scalar(out=res[:, 2:4, :], in0=acc[:], scalar1=OUT_SCALE, scalar2=0.0, op0=ALU.mult, op1=ALU.add)
+            queue.dma_start(out=out_rows[:, :, j0 : j0 + n], in_=res[:])
+            return res
+
+        def hand_on(j0, n, res_woven, tag=None):
+            ow = keep.tile([P, n], U32, name="ow%d" % j0, tag=tag or "ow%d" % j0, align_bytes=64)
+            nc.vector.quantize_mx(
+                out=ow[:].bitcast(FP8X4), scales=out_scales[:, j0 : j0 + n], in_=res_woven[:].rearrange("p n t -> p (n t)")
+            )
+            nc.sync.dma_start(out=words_of(out_1)[:, j0 : j0 + n], in_=ow[:].bitcast(I32))
+
+        every = slice(0, P)
+
+        def row(e):
+            return (every, e, slice(0, CHUNK))
+
+        def cols(c0, c1):
+            return (every, slice(0, 2), slice(c0, c1))
+
+        def up_to_over(u, n2_tag=None, abs_tag=None):
+            fetch_n2(u, n2_tag)
+            fetch_gap(u, 0.5, None, abs_tag)
+            make_low(u)
+            new_rows("over", u)
+            for e in range(2):
+                fetch_over(u, e)
+
+        def gains(u, tag=None):
+            new_rows("gain", u, tag)
+            new_rows("gain_abs", u)
+            for e in range(2):
+                nc.vector.scalar_tensor_tensor(
+                    out=part("gain", u, e), in0=part("over", u, e), scalar=0.5, in1=part("gap_abs", u, e), op0=ALU.mult, op1=ALU.min
+                )
+                nc.scalar.activation(out=part("gain_abs", u, e), in_=part("gain", u, e), func=ACT.Abs)
+
+        dw_pick = keep.tile([P, H], U32, name="dw_pick", align_bytes=64)
+        nc.vector.tensor_copy(out=dw_pick[:], in_=dw_win[:].indirect(kq_sb[:]))
+        up_to_over(0)
+        gains(0)
+        sig_by_transposes(0, (5, 6, 7, 0))
+        up_to_over(1, "over0", "sig_turned0")
+        deal(dw[:].bitcast(I32), dw_pick[:].bitcast(I32))
+        weigh(0, gs2)
+        gains(1, "gain_abs0")
+        sig_by_transposes(1, (5, 6, 7, 0))
+        up_to_over(2, "over1", "sig_turned1")
+        weigh(1, gs2)
+        gains(2, "gain_abs1")
+        z_woven = weave(nc.scalar.copy, z[0][:], "z_woven0", "sig_turned1")
+        sig_by_transposes(2, (5, 6, 7, 0))
+        fetch_n2(3, "over2")
+        zq = quantise_z(0, CHUNK, z_woven)
+        fetch_gap(3, 1.0)
+        make_low(3, "sig_turned1")
+        res_woven_a, accs_a = second_product(0, CHUNK, zq, (1, 2))
+        for name in ("over", "gain", "neg_md"):
+            new(name, 3)
+        factors = keep.tile([P, 2, 2, CHUNK], F32, name="factors", tag="sig_turned2", align_bytes=64)
+        st["gain_abs", 3], st["sig", 3] = factors[:, 0], factors[:, 1]
+        for e in range(2):
+            fetch_over(3, e)
+        for e in range(2):
+            make_gain(3, 1.0, row(e))
+        for e in range(2):
+            sig_direct(3, row(e))
+        store_result(0, accs_a, "neg_md3")
+        weigh(2, gs2)
+        weigh(3, gs_sb)
+        z_woven_b = weave(nc.vector.tensor_copy, z[1][:, :, 0:SUB], "z_woven256")
+        z_woven_c = weave(nc.vector.tensor_copy, z[1][:, :, SUB:CHUNK], "z_woven384")
+        zq_b = quantise_z(CHUNK, SUB, z_woven_b)
+        zq_c = quantise_z(CHUNK + SUB, SUB, z_woven_c)
+        hand_on(0, CHUNK, res_woven_a, "z_woven256")
+        res_b = last_product(CHUNK, SUB, zq_b, (3, 5), nc.sync)
+        res_c = last_product(CHUNK + SUB, SUB, zq_c, (4, 6), nc.sync)
+        res_woven_b = weave(nc.scalar.copy, res_b[:], "res_woven256")
+        res_woven_c = weave(nc.vector.tensor_copy, res_c[:], "res_woven384")
+        hand_on(CHUNK, SUB, res_woven_b)
+        hand_on(CHUNK + SUB, SUB, res_woven_c)
         for q in range(4):
             eng = nc.scalar if q % 2 else nc.sync
             eng.dma_start(out=out_2[0].bitcast(I32)[4 * q : 4 * q + 4, :], in_=out_scales[32 * q : 32 * q + 4, :].bitcast(I32))

@@ -53,11 +53,9 @@ def tile_picked_auction2_none_po_kernel(
         xw = keep.tile([P, S], U32, name="xw", align_bytes=64)
         xs = keep.tile([P, S], U8, name="xs", align_bytes=64)
         ds_pick = keep.tile([P, H], U8, name="ds_pick", align_bytes=64)
-        dw = keep.tile([P, H], U32, name="dw", align_bytes=64)
         ds = keep.tile([P, H], U8, name="ds", align_bytes=64)
         out_scales = keep.tile([P, S], U8, name="out_scales", align_bytes=64)
         gs_sb = keep.tile([P, PACK], F32, name="gs_sb")
-        gs2 = keep.tile([P, PACK], F32, name="gs2")
 
         def deal(dst, src):
             nc.vector.tensor_copy(out=dst.rearrange("p (t m) -> p m t", t=PACK), in_=src.rearrange("p (m t) -> p m t", t=PACK))
@@ -120,10 +118,9 @@ def tile_picked_auction2_none_po_kernel(
                 stop=True,
             )
             nc.scalar.activation(out=neg_y[t][:, j0 : j0 + n], in_=acc[:], func=ACT.Copy, scale=-1.0)
-        nc.scalar.activation(out=gs2[:], in_=gs_sb[:], func=ACT.Copy, scale=2.0)
 
         st = {}
-        z = [keep.tile([P, PACK, CHUNK], BF16, name="z%d" % c, align_bytes=64) for c in range(2)]
+        z = [keep.tile([P, PACK, CHUNK], BF16, name="z%d" % c, tag="z%d" % c, align_bytes=64) for c in range(2)]
         out_rows = out_0.rearrange("(p t) j -> p t j", t=PACK)
 
         def new(name, u, tag=None):
@@ -173,20 +170,46 @@ def tile_picked_auction2_none_po_kernel(
             )
             nc.scalar.activation(out=st["gain_abs", u][at], in_=st["gain", u][at], func=ACT.Abs)
 
-        def sig_by_transposes(u, banks):
-            sig_turned = keep.tile([P, 2, CHUNK], F32, name="sig_turned%d" % u, tag="sig_turned%d" % u, align_bytes=64)
+        def turn(dst, *terms):
+            for c0 in range(0, CHUNK, P):
+                for i, term in enumerate(terms):
+                    nc.tensor.matmul(
+                        out=dst[:, c0 : c0 + P], lhsT=term[:, c0 : c0 + P], rhs=ident[:], is_transpose=True, start=i == 0, stop=i == len(terms) - 1
+                    )
+
+        def fetch_differences(u, n2_tag=None, high_tag=None, over_tag=None):
+            fetch_n2(u, n2_tag)
+            gap = new("gap", u)
+            new_rows("over", u, over_tag)
             for e in range(2):
-                turned = bank(banks[e], [P, CHUNK], "turned")
-                for c0 in range(0, CHUNK, P):
-                    for i, name in enumerate(("low", "gain", "gain_abs")):
-                        nc.tensor.matmul(
-                            out=turned[:, c0 : c0 + P], lhsT=part(name, u, e, c0, c0 + P), rhs=ident[:], is_transpose=True, start=i == 0, stop=i == 2
-                        )
-                nc.scalar.activation(out=sig_turned[:, e, :], in_=turned[:], func=ACT.Sigmoid, scale=-1.0)
-            st["sig", u] = [bank(banks[2 + e], [P, CHUNK], "sig") for e in range(2)]
+                nc.vector.tensor_tensor(out=gap[:, e, :], in0=picked(b1_sb, u, e), in1=part("n2", u, e), op=ALU.subtract)
+            nc.scalar.activation(out=new("high", u, high_tag)[:], in_=gap[:], func=ACT.Relu, scale=-1.0)
             for e in range(2):
-                for c0 in range(0, CHUNK, P):
-                    nc.tensor.transpose(part("sig", u, e, c0, c0 + P), sig_turned[:, e, c0 : c0 + P], ident[:])
+                nc.vector.tensor_tensor(out=part("over", u, e), in0=picked(b3_sb, u, e), in1=part("n2", u, e), op=ALU.subtract)
+
+        def make_rest(u):
+            new_rows("rest", u)
+            for e in range(2):
+                nc.vector.scalar_tensor_tensor(
+                    out=part("rest", u, e), in0=part("gap", u, e), scalar=0.0, in1=part("over", u, e), op0=ALU.max, op1=ALU.min
+                )
+
+        def factors_by_transposes(u, banks):
+            turned = [keep.tile([P, 3, CHUNK], F32, name="turned%d_%d" % (u, e), tag="turned%d_%d" % (u, e), align_bytes=64) for e in range(2)]
+            for e in range(2):
+                sums = bank(banks[e], [P, 2, CHUNK], "sums")
+                turn(sums[:, 1, :], part("n2", u, e), part("rest", u, e))
+                turn(sums[:, 0, :], part("high", u, e), part("rest", u, e))
+                nc.scalar.activation(out=turned[e][:, 0, :], in_=sums[:, 0, :], func=ACT.Relu, scale=-1.0)
+                nc.scalar.activation(out=turned[e][:, 1, :], in_=sums[:, 1, :], func=ACT.Copy)
+                nc.scalar.activation(out=turned[e][:, 2, :], in_=sums[:, 0, :], func=ACT.Abs)
+            new_rows("sig", u)
+            neg_md, st["gain_abs", u] = bank(banks[2], [P, 2, CHUNK], "neg_md"), bank(banks[3], [P, 2, CHUNK], "gain_abs")
+            for e in range(2):
+                turn(neg_md[:, e, :], turned[e][:, 0, :], turned[e][:, 1, :])
+                turn(part("gain_abs", u, e), turned[e][:, 2, :])
+            for e in range(2):
+                nc.scalar.activation(out=part("sig", u, e), in_=neg_md[:, e, :], func=ACT.Sigmoid, scale=-1.0)
 
         def sig_direct(u, at):
             nc.vector.scalar_tensor_tensor(
@@ -226,17 +249,21 @@ def tile_picked_auction2_none_po_kernel(
 
         def second_product(j0, n, zq, banks):
             zw, zs = zq
-            res_woven = keep.tile([P, n, PACK], BF16, name="res_woven%d" % j0, align_bytes=64)
             accs = []
             for s0, b in zip(range(0, n, SUB), banks):
                 acc = bank(b, [P, PACK, SUB], "o_acc")
                 for t in range(PACK):
                     product(acc[:, t, :], t, zw[:, s0 : s0 + SUB], zs[:, s0 : s0 + SUB])
-                nc.scalar.activation(
-                    out=res_woven[:, s0 : s0 + SUB, :], in_=acc[:].rearrange("p t n -> p n t"), func=ACT.Copy, scale=OUT_SCALE
-                )
                 accs.append(acc)
-            return res_woven, accs
+            return accs
+
+        def weave_result(j0, accs, tag):
+            woven = keep.tile([P, SUB * len(accs), PACK], BF16, name="res_woven%d" % j0, tag=tag, align_bytes=64)
+            for i, acc in enumerate(accs):
+                nc.scalar.activation(
+                    out=woven[:, i * SUB : (i + 1) * SUB, :], in_=acc[:].rearrange("p t n -> p n t"), func=ACT.Copy, scale=OUT_SCALE
+                )
+            return woven
 
         def store_result(j0, accs, tag):
             res = keep.tile([P, PACK, SUB * len(accs)], F32, name="res%d" % j0, tag=tag, align_bytes=64)
@@ -292,27 +319,29 @@ def tile_picked_auction2_none_po_kernel(
 
         dw_pick = keep.tile([P, H], U32, name="dw_pick", align_bytes=64)
         nc.vector.tensor_copy(out=dw_pick[:], in_=dw_win[:].indirect(kq_sb[:]))
-        up_to_over(0)
-        gains(0)
-        sig_by_transposes(0, (5, 6, 7, 0))
-        up_to_over(1, "over0", "sig_turned0")
+        fetch_differences(0)
+        make_rest(0)
+        factors_by_transposes(0, (5, 6, 7, 0))
+        fetch_differences(1, "over0", "turned0_0")
+        make_rest(1)
+        factors_by_transposes(1, (5, 6, 3, 4))
+        fetch_differences(2, "over1", "turned1_0")
+        make_rest(2)
+        weigh(0, gs_sb)
+        weigh(1, gs_sb)
+        dw = keep.tile([P, H], U32, name="dw", tag="sig1_0", align_bytes=64)
         deal(dw[:].bitcast(I32), dw_pick[:].bitcast(I32))
-        weigh(0, gs2)
-        gains(1, "gain_abs0")
-        sig_by_transposes(1, (5, 6, 7, 0))
-        up_to_over(2, "over1", "sig_turned1")
-        weigh(1, gs2)
-        gains(2, "gain_abs1")
-        z_woven = weave(nc.scalar.copy, z[0][:], "z_woven0", "sig_turned1")
-        sig_by_transposes(2, (5, 6, 7, 0))
-        fetch_n2(3, "over2")
+        factors_by_transposes(2, (5, 6, 7, 0))
+        z_woven = weave(nc.scalar.copy, z[0][:], "z_woven0", "rest2_0")
+        fetch_n2(3, "sig0")
+        fetch_gap(3, 1.0, "sig1_1", "rest2_1")
+        make_low(3)
         zq = quantise_z(0, CHUNK, z_woven)
-        fetch_gap(3, 1.0)
-        make_low(3, "sig_turned1")
-        res_woven_a, accs_a = second_product(0, CHUNK, zq, (1, 2))
-        for name in ("over", "gain", "neg_md"):
-            new(name, 3)
-        factors = keep.tile([P, 2, 2, CHUNK], F32, name="factors", tag="sig_turned2", align_bytes=64)
+        accs_a = second_product(0, CHUNK, zq, (1, 2))
+        new("over", 3, "z0")
+        new("gain", 3)
+        new("neg_md", 3)
+        factors = keep.tile([P, 2, 2, CHUNK], F32, name="factors", tag="turned2_1", align_bytes=64)
         st["gain_abs", 3], st["sig", 3] = factors[:, 0], factors[:, 1]
         for e in range(2):
             fetch_over(3, e)
@@ -320,9 +349,10 @@ def tile_picked_auction2_none_po_kernel(
             make_gain(3, 1.0, row(e))
         for e in range(2):
             sig_direct(3, row(e))
-        store_result(0, accs_a, "neg_md3")
-        weigh(2, gs2)
+        res_woven_a = weave_result(0, accs_a, "neg_md3")
+        weigh(2, gs_sb)
         weigh(3, gs_sb)
+        store_result(0, accs_a, "turned2_1")
         z_woven_b = weave(nc.vector.tensor_copy, z[1][:, :, 0:SUB], "z_woven256")
         z_woven_c = weave(nc.vector.tensor_copy, z[1][:, :, SUB:CHUNK], "z_woven384")
         zq_b = quantise_z(CHUNK, SUB, z_woven_b)
@@ -332,8 +362,12 @@ def tile_picked_auction2_none_po_kernel(
         res_c = last_product(CHUNK + SUB, SUB, zq_c, (4, 6), nc.sync)
         res_woven_b = weave(nc.scalar.copy, res_b[:], "res_woven256")
         res_woven_c = weave(nc.vector.tensor_copy, res_c[:], "res_woven384")
-        hand_on(CHUNK, SUB, res_woven_b)
-        hand_on(CHUNK + SUB, SUB, res_woven_c)
+        ow = keep.tile([P, CHUNK], U32, name="ow_last", align_bytes=64)
+        for s0, woven in ((0, res_woven_b), (SUB, res_woven_c)):
+            nc.vector.quantize_mx(
+                out=ow[:, s0 : s0 + SUB].bitcast(FP8X4), scales=out_scales[:, CHUNK + s0 : CHUNK + s0 + SUB], in_=woven[:].rearrange("p n t -> p (n t)")
+            )
+        nc.sync.dma_start(out=words_of(out_1)[:, CHUNK:], in_=ow[:].bitcast(I32))
         for q in range(4):
             eng = nc.scalar if q % 2 else nc.sync
             eng.dma_start(out=out_2[0].bitcast(I32)[4 * q : 4 * q + 4, :], in_=out_scales[32 * q : 32 * q + 4, :].bitcast(I32))

@@ -15,13 +15,14 @@ ACT = mybir.ActivationFunctionType
 
 P = 128
 PACK = 4
+GROUP = 16
 K, T, S, H, G = 512, 2048, 512, 512, 2048
 FLOPS = 2 * K * H * S + 2 * H * H * S
 OUT_SCALE = 0.0625
-SUB = 128
-UNITS = (((0, 1), 0), ((2, 3), 0), ((0, 1), 256), ((2, 3), 256))
 CHUNK = 256
-WIDTH = 512
+SUB = 128
+UNITS = (((0, 1), 0), ((2, 3), 0), ((0, 1), CHUNK), ((2, 3), CHUNK))
+LAST = len(UNITS) - 1
 
 
 def tile_picked_auction2_none_po_kernel(
@@ -36,18 +37,18 @@ def tile_picked_auction2_none_po_kernel(
         keep = ctx.enter_context(tc.tile_pool(name="keep", bufs=1))
         psum = ctx.enter_context(tc.psum_pool(name="psum", bufs=1))
 
-        offs_sb = keep.tile([P, S // 16], U16, name="offs_sb")
-        b1_sb = keep.tile([P, S // 16], U16, name="b1_sb")
-        b2_sb = keep.tile([P, S // 16], U16, name="b2_sb")
-        b3_sb = keep.tile([P, S // 16], U16, name="b3_sb")
-        kq_sb = keep.tile([P, H // 16], U16, name="kq_sb")
+        offs_sb = keep.tile([P, S // GROUP], U16, name="offs_sb")
+        b1_sb = keep.tile([P, S // GROUP], U16, name="b1_sb")
+        b2_sb = keep.tile([P, S // GROUP], U16, name="b2_sb")
+        b3_sb = keep.tile([P, S // GROUP], U16, name="b3_sb")
+        kq_sb = keep.tile([P, H // GROUP], U16, name="kq_sb")
 
         xw_win = keep.tile([P, T], U32, name="xw_win", align_bytes=64)
         dw_win = keep.tile([P, G], U32, name="dw_win", align_bytes=64)
         xs_win = keep.tile([P, T], U8, name="xs_win", align_bytes=64)
         ds_win = keep.tile([P, G], U8, name="ds_win", align_bytes=64)
         w1w_raw = keep.tile([P, H], U32, name="w1w_raw", align_bytes=64)
-        w1s_raw = keep.tile([P, H], U8, name="w1s_raw", tag="scales_to_deal", align_bytes=64)
+        w1s_raw = keep.tile([P, H], U8, name="w1s_raw", tag="w1s_raw", align_bytes=64)
         w1w = keep.tile([P, H], U32, name="w1w", align_bytes=64)
         w1s = keep.tile([P, H], U8, name="w1s", align_bytes=64)
         xw = keep.tile([P, S], U32, name="xw", align_bytes=64)
@@ -63,13 +64,9 @@ def tile_picked_auction2_none_po_kernel(
         def bank(i, shape, name):
             return psum.tile(shape, F32, name=name, tag="bank%d" % i)
 
-        warm_in = keep.tile([P, 1], F32, name="warm_in")
-        warm_out = keep.tile([P, 1], F32, name="warm_out")
-        nc.vector.memset(warm_in[:], 0.0)
-        nc.scalar.activation(out=warm_out[:], in_=warm_in[:], func=ACT.Sigmoid)
         nc.vector.memset(ds_win[:].bitcast(I32), 0)
-        for plane in (xs_win, w1s_raw, ds):
-            nc.gpsimd.memset(plane[:].bitcast(I32), 0)
+        for scale_tile in (xs_win, w1s_raw, ds):
+            nc.gpsimd.memset(scale_tile[:].bitcast(I32), 0)
         ident = keep.tile([P, P], F32, name="ident", align_bytes=64)
         make_identity(nc, ident[:])
 
@@ -92,15 +89,16 @@ def tile_picked_auction2_none_po_kernel(
         w1_moves = ((w1w[:].bitcast(I32), w1w_raw[:].bitcast(I32)), (w1s[:], w1s_raw[:]))
         nc.vector.tensor_copy(out=xs[:], in_=xs_win[:].indirect(offs_sb[:]))
         nc.vector.tensor_copy(out=ds_pick[:], in_=ds_win[:].indirect(kq_sb[:]))
-        for h in range(2):
-            nc.vector.tensor_copy(out=xw[:, h * half : (h + 1) * half], in_=xw_win[:].indirect(offs_sb[:, h * half // 16 : (h + 1) * half // 16]))
+        for j0 in (0, half):
+            entries = offs_sb[:, j0 // GROUP : (j0 + half) // GROUP]
+            nc.vector.tensor_copy(out=xw[:, j0 : j0 + half], in_=xw_win[:].indirect(entries))
         for dst, src in w1_moves:
             nc.vector.tensor_copy(out=dst[:, :P], in_=src.rearrange("p (m t) -> p m t", t=PACK)[:, :, 0])
         for dst, src in w1_moves:
             nc.vector.tensor_copy(
                 out=dst[:, P:].rearrange("p (t m) -> p m t", t=PACK - 1), in_=src.rearrange("p (m t) -> p m t", t=PACK)[:, :, 1:]
             )
-        ds_dealt = keep.tile([P, H], U8, name="ds_dealt", tag="scales_to_deal", align_bytes=64)
+        ds_dealt = keep.tile([P, H], U8, name="ds_dealt", tag="w1s_raw", align_bytes=64)
         deal(ds_dealt[:], ds_pick[:])
         for r in range(4):
             nc.sync.dma_start(out=ds[r:P:32, :].bitcast(I32), in_=ds_dealt[8 * r : P : 32, :].bitcast(I32))
@@ -119,56 +117,39 @@ def tile_picked_auction2_none_po_kernel(
             )
             nc.scalar.activation(out=neg_y[t][:, j0 : j0 + n], in_=acc[:], func=ACT.Copy, scale=-1.0)
 
-        st = {}
-        z = [keep.tile([P, PACK, CHUNK], BF16, name="z%d" % c, tag="z%d" % c, align_bytes=64) for c in range(2)]
+        vals = {}
+        z = [keep.tile([P, PACK, CHUNK], BF16, name="z%d" % c, tag="z%d" % c, align_bytes=64) for c in range(S // CHUNK)]
         out_rows = out_0.rearrange("(p t) j -> p t j", t=PACK)
 
-        def new(name, u, tag=None):
-            st[name, u] = keep.tile([P, 2, CHUNK], F32, name="%s%d" % (name, u), tag=tag or "%s%d" % (name, u), align_bytes=64)
-            return st[name, u]
+        def new(name, u, after=None):
+            vals[name, u] = keep.tile([P, 2, CHUNK], F32, name="%s%d" % (name, u), tag=after or "%s%d" % (name, u), align_bytes=64)
+            return vals[name, u]
 
-        def new_rows(name, u, tag=None):
-            st[name, u] = [
-                keep.tile([P, CHUNK], F32, name="%s%d_%d" % (name, u, e), tag="%s_%d" % (tag or "%s%d" % (name, u), e), align_bytes=64)
+        def new_rows(name, u, after=None):
+            vals[name, u] = [
+                keep.tile([P, CHUNK], F32, name="%s%d_%d" % (name, u, e), tag="%s_%d" % (after or "%s%d" % (name, u), e), align_bytes=64)
                 for e in range(2)
             ]
 
-        def part(name, u, e, c0=0, c1=CHUNK):
-            held = st[name, u]
-            return held[e][:, c0:c1] if isinstance(held, list) else held[:, e, c0:c1]
+        def part(name, u, e):
+            held = vals[name, u]
+            return held[e][:] if isinstance(held, list) else held[:, e, :]
 
-        def picked(lst, u, e, c0=0, c1=CHUNK):
+        def picked(lst, u, e):
             ts, j0 = UNITS[u]
-            return neg_y[ts[e]][:].indirect(lst[:, (j0 + c0) // 16 : (j0 + c1) // 16])
+            return neg_y[ts[e]][:].indirect(lst[:, j0 // GROUP : (j0 + CHUNK) // GROUP])
 
-        def fetch_n2(u, tag=None):
-            new_rows("n2", u, tag)
+        def fetch_neg_x2(u, after=None):
+            new_rows("neg_x2_", u, after)
             for e in range(2):
-                nc.vector.tensor_copy(out=part("n2", u, e), in_=picked(b2_sb, u, e))
+                nc.vector.tensor_copy(out=part("neg_x2_", u, e), in_=picked(b2_sb, u, e))
 
-        def fetch_gap(u, factor, tag=None, abs_tag=None):
-            gap, gap_abs = new("gap", u, tag), new("gap_abs", u, abs_tag)
+        def fetch_less(name, lst, base, u):
             for e in range(2):
-                nc.vector.tensor_tensor(out=gap[:, e, :], in0=picked(b1_sb, u, e), in1=part("n2", u, e), op=ALU.subtract)
-            nc.scalar.activation(out=gap_abs[:], in_=gap[:], func=ACT.Abs, scale=factor)
+                nc.vector.tensor_tensor(out=part(name, u, e), in0=picked(lst, u, e), in1=part(base, u, e), op=ALU.subtract)
 
-        def make_low(u, tag=None):
-            low = new("low", u, tag)
-            for e in range(2):
-                nc.vector.scalar_tensor_tensor(
-                    out=low[:, e, :], in0=st["gap", u][:, e, :], scalar=0.0, in1=part("n2", u, e), op0=ALU.min, op1=ALU.add
-                )
-
-        def fetch_over(u, e, c0=0, c1=CHUNK):
-            nc.vector.tensor_tensor(
-                out=part("over", u, e, c0, c1), in0=picked(b3_sb, u, e, c0, c1), in1=st["low", u][:, e, c0:c1], op=ALU.subtract
-            )
-
-        def make_gain(u, factor, at):
-            nc.vector.scalar_tensor_tensor(
-                out=st["gain", u][at], in0=st["over", u][at], scalar=factor, in1=st["gap_abs", u][at], op0=ALU.mult, op1=ALU.min
-            )
-            nc.scalar.activation(out=st["gain_abs", u][at], in_=st["gain", u][at], func=ACT.Abs)
+        def combine(name, in0, scalar, op0, op1, in1, u, e):
+            nc.vector.scalar_tensor_tensor(out=part(name, u, e), in0=part(in0, u, e), scalar=scalar, in1=part(in1, u, e), op0=op0, op1=op1)
 
         def turn(dst, *terms):
             for c0 in range(0, CHUNK, P):
@@ -177,63 +158,55 @@ def tile_picked_auction2_none_po_kernel(
                         out=dst[:, c0 : c0 + P], lhsT=term[:, c0 : c0 + P], rhs=ident[:], is_transpose=True, start=i == 0, stop=i == len(terms) - 1
                     )
 
-        def fetch_differences(u, n2_tag=None, high_tag=None, over_tag=None):
-            fetch_n2(u, n2_tag)
-            gap = new("gap", u)
-            new_rows("over", u, over_tag)
+        def order_bids(u, x2_after=None, lead_after=None):
+            fetch_neg_x2(u, x2_after)
+            d21 = new("d21_", u)
+            new_rows("d23_", u)
+            fetch_less("d21_", b1_sb, "neg_x2_", u)
+            nc.scalar.activation(out=new("lead", u, lead_after)[:], in_=d21[:], func=ACT.Relu, scale=-1.0)
+            fetch_less("d23_", b3_sb, "neg_x2_", u)
+            new_rows("lag", u)
             for e in range(2):
-                nc.vector.tensor_tensor(out=gap[:, e, :], in0=picked(b1_sb, u, e), in1=part("n2", u, e), op=ALU.subtract)
-            nc.scalar.activation(out=new("high", u, high_tag)[:], in_=gap[:], func=ACT.Relu, scale=-1.0)
-            for e in range(2):
-                nc.vector.tensor_tensor(out=part("over", u, e), in0=picked(b3_sb, u, e), in1=part("n2", u, e), op=ALU.subtract)
-
-        def make_rest(u):
-            new_rows("rest", u)
-            for e in range(2):
-                nc.vector.scalar_tensor_tensor(
-                    out=part("rest", u, e), in0=part("gap", u, e), scalar=0.0, in1=part("over", u, e), op0=ALU.max, op1=ALU.min
-                )
+                combine("lag", "d21_", 0.0, ALU.max, ALU.min, "d23_", u, e)
 
         def factors_by_transposes(u, banks):
             turned = [keep.tile([P, 3, CHUNK], F32, name="turned%d_%d" % (u, e), tag="turned%d_%d" % (u, e), align_bytes=64) for e in range(2)]
             for e in range(2):
                 sums = bank(banks[e], [P, 2, CHUNK], "sums")
-                turn(sums[:, 1, :], part("n2", u, e), part("rest", u, e))
-                turn(sums[:, 0, :], part("high", u, e), part("rest", u, e))
-                nc.scalar.activation(out=turned[e][:, 0, :], in_=sums[:, 0, :], func=ACT.Relu, scale=-1.0)
-                nc.scalar.activation(out=turned[e][:, 1, :], in_=sums[:, 1, :], func=ACT.Copy)
-                nc.scalar.activation(out=turned[e][:, 2, :], in_=sums[:, 0, :], func=ACT.Abs)
+                gain, neg_rival = sums[:, 0, :], sums[:, 1, :]
+                turn(neg_rival, part("neg_x2_", u, e), part("lag", u, e))
+                turn(gain, part("lead", u, e), part("lag", u, e))
+                nc.scalar.activation(out=turned[e][:, 0, :], in_=gain, func=ACT.Relu, scale=-1.0)
+                nc.scalar.activation(out=turned[e][:, 1, :], in_=neg_rival, func=ACT.Copy)
+                nc.scalar.activation(out=turned[e][:, 2, :], in_=gain, func=ACT.Abs)
             new_rows("sig", u)
-            neg_md, st["gain_abs", u] = bank(banks[2], [P, 2, CHUNK], "neg_md"), bank(banks[3], [P, 2, CHUNK], "gain_abs")
+            neg_md, vals["gain_abs", u] = bank(banks[2], [P, 2, CHUNK], "neg_md"), bank(banks[3], [P, 2, CHUNK], "gain_abs")
             for e in range(2):
                 turn(neg_md[:, e, :], turned[e][:, 0, :], turned[e][:, 1, :])
                 turn(part("gain_abs", u, e), turned[e][:, 2, :])
             for e in range(2):
                 nc.scalar.activation(out=part("sig", u, e), in_=neg_md[:, e, :], func=ACT.Sigmoid, scale=-1.0)
 
-        def sig_direct(u, at):
-            nc.vector.scalar_tensor_tensor(
-                out=st["neg_md", u][at], in0=st["gain", u][at], scalar=0.0, in1=st["low", u][at], op0=ALU.max, op1=ALU.add
-            )
-            nc.scalar.activation(out=st["sig", u][at], in_=st["neg_md", u][at], func=ACT.Sigmoid, scale=-1.0)
-
-        def weigh(u, weight, c0=0, c1=CHUNK):
+        def weigh(u):
             ts, j0 = UNITS[u]
             for e, t in enumerate(ts):
                 nc.vector.scalar_tensor_tensor(
-                    out=z[j0 // CHUNK][:, t, c0:c1], in0=part("gain_abs", u, e, c0, c1), scalar=weight[:, t : t + 1],
-                    in1=part("sig", u, e, c0, c1), op0=ALU.mult, op1=ALU.mult,
+                    out=z[j0 // CHUNK][:, t, :], in0=part("gain_abs", u, e), scalar=gs_sb[:, t : t + 1], in1=part("sig", u, e),
+                    op0=ALU.mult, op1=ALU.mult,
                 )
 
-        def weave(copy, src, name, tag=None):
-            woven = keep.tile([P, src.shape[2], PACK], BF16, name=name, tag=tag or name, align_bytes=64)
+        def weave(copy, src, name, after=None):
+            woven = keep.tile([P, src.shape[2], PACK], BF16, name=name, tag=after or name, align_bytes=64)
             copy(out=woven[:], in_=src.rearrange("p t n -> p n t"))
             return woven
 
-        def quantise_z(j0, n, z_woven):
-            zw = keep.tile([P, n], U32, name="zw%d" % j0, align_bytes=64)
-            zs = keep.tile([P, n], U8, name="zs%d" % j0, align_bytes=64)
-            nc.vector.quantize_mx(out=zw[:].bitcast(FP8X4), scales=zs[:], in_=z_woven[:].rearrange("p n t -> p (n t)"))
+        def quantise(words, scales, woven):
+            nc.vector.quantize_mx(out=words.bitcast(FP8X4), scales=scales, in_=woven[:].rearrange("p n t -> p (n t)"))
+
+        def quantise_z(j0, woven):
+            zw = keep.tile([P, woven[:].shape[1]], U32, name="zw%d" % j0, align_bytes=64)
+            zs = keep.tile([P, woven[:].shape[1]], U8, name="zs%d" % j0, align_bytes=64)
+            quantise(zw[:], zs[:], woven)
             return zw, zs
 
         def product(out, t, zw, zs):
@@ -247,127 +220,89 @@ def tile_picked_auction2_none_po_kernel(
                 stop=True,
             )
 
-        def second_product(j0, n, zq, banks):
-            zw, zs = zq
-            accs = []
-            for s0, b in zip(range(0, n, SUB), banks):
-                acc = bank(b, [P, PACK, SUB], "o_acc")
-                for t in range(PACK):
-                    product(acc[:, t, :], t, zw[:, s0 : s0 + SUB], zs[:, s0 : s0 + SUB])
-                accs.append(acc)
-            return accs
-
-        def weave_result(j0, accs, tag):
-            woven = keep.tile([P, SUB * len(accs), PACK], BF16, name="res_woven%d" % j0, tag=tag, align_bytes=64)
-            for i, acc in enumerate(accs):
-                nc.scalar.activation(
-                    out=woven[:, i * SUB : (i + 1) * SUB, :], in_=acc[:].rearrange("p t n -> p n t"), func=ACT.Copy, scale=OUT_SCALE
-                )
-            return woven
-
-        def store_result(j0, accs, tag):
-            res = keep.tile([P, PACK, SUB * len(accs)], F32, name="res%d" % j0, tag=tag, align_bytes=64)
-            for i, acc in enumerate(accs):
-                nc.scalar.activation(out=res[:, :, i * SUB : (i + 1) * SUB], in_=acc[:], func=ACT.Copy, scale=OUT_SCALE)
-            nc.sync.dma_start(out=out_rows[:, :, j0 : j0 + SUB * len(accs)], in_=res[:])
-
-        def last_product(j0, n, zq, banks, queue):
-            zw, zs = zq
-            res = keep.tile([P, PACK, n], F32, name="res%d" % j0, align_bytes=64)
+        def closing_product(j0, zw, zs, banks):
+            res = keep.tile([P, PACK, SUB], F32, name="res%d" % j0, align_bytes=64)
             for i, b in enumerate(banks):
-                acc = bank(b, [P, 2, n], "o_acc")
+                acc = bank(b, [P, 2, SUB], "o_acc")
                 for e in range(2):
                     product(acc[:, e, :], 2 * i + e, zw[:], zs[:])
                 if i == 0:
                     nc.scalar.activation(out=res[:, 0:2, :], in_=acc[:], func=ACT.Copy, scale=OUT_SCALE)
                 else:
                     nc.vector.tensor_scalar(out=res[:, 2:4, :], in0=acc[:], scalar1=OUT_SCALE, scalar2=0.0, op0=ALU.mult, op1=ALU.add)
-            queue.dma_start(out=out_rows[:, :, j0 : j0 + n], in_=res[:])
+            nc.sync.dma_start(out=out_rows[:, :, j0 : j0 + SUB], in_=res[:])
             return res
-
-        def hand_on(j0, n, res_woven, tag=None):
-            ow = keep.tile([P, n], U32, name="ow%d" % j0, tag=tag or "ow%d" % j0, align_bytes=64)
-            nc.vector.quantize_mx(
-                out=ow[:].bitcast(FP8X4), scales=out_scales[:, j0 : j0 + n], in_=res_woven[:].rearrange("p n t -> p (n t)")
-            )
-            nc.sync.dma_start(out=words_of(out_1)[:, j0 : j0 + n], in_=ow[:].bitcast(I32))
-
-        every = slice(0, P)
-
-        def row(e):
-            return (every, e, slice(0, CHUNK))
-
-        def cols(c0, c1):
-            return (every, slice(0, 2), slice(c0, c1))
-
-        def up_to_over(u, n2_tag=None, abs_tag=None):
-            fetch_n2(u, n2_tag)
-            fetch_gap(u, 0.5, None, abs_tag)
-            make_low(u)
-            new_rows("over", u)
-            for e in range(2):
-                fetch_over(u, e)
-
-        def gains(u, tag=None):
-            new_rows("gain", u, tag)
-            new_rows("gain_abs", u)
-            for e in range(2):
-                nc.vector.scalar_tensor_tensor(
-                    out=part("gain", u, e), in0=part("over", u, e), scalar=0.5, in1=part("gap_abs", u, e), op0=ALU.mult, op1=ALU.min
-                )
-                nc.scalar.activation(out=part("gain_abs", u, e), in_=part("gain", u, e), func=ACT.Abs)
 
         dw_pick = keep.tile([P, H], U32, name="dw_pick", align_bytes=64)
         nc.vector.tensor_copy(out=dw_pick[:], in_=dw_win[:].indirect(kq_sb[:]))
-        fetch_differences(0)
-        make_rest(0)
+
+        order_bids(0)
         factors_by_transposes(0, (5, 6, 7, 0))
-        fetch_differences(1, "over0", "turned0_0")
-        make_rest(1)
+        order_bids(1, x2_after="d23_0", lead_after="turned0_0")
         factors_by_transposes(1, (5, 6, 3, 4))
-        fetch_differences(2, "over1", "turned1_0")
-        make_rest(2)
-        weigh(0, gs_sb)
-        weigh(1, gs_sb)
+        order_bids(2, x2_after="d23_1", lead_after="turned1_0")
+        weigh(0)
+        weigh(1)
         dw = keep.tile([P, H], U32, name="dw", tag="sig1_0", align_bytes=64)
         deal(dw[:].bitcast(I32), dw_pick[:].bitcast(I32))
         factors_by_transposes(2, (5, 6, 7, 0))
-        z_woven = weave(nc.scalar.copy, z[0][:], "z_woven0", "rest2_0")
-        fetch_n2(3, "sig0")
-        fetch_gap(3, 1.0, "sig1_1", "rest2_1")
-        make_low(3)
-        zq = quantise_z(0, CHUNK, z_woven)
-        accs_a = second_product(0, CHUNK, zq, (1, 2))
-        new("over", 3, "z0")
-        new("gain", 3)
-        new("neg_md", 3)
+
+        z_woven = weave(nc.scalar.copy, z[0][:], "z_woven0", after="lag2_0")
+        fetch_neg_x2(LAST, after="sig0")
+        d21, d21_abs = new("d21_", LAST, after="sig1_1"), new("d21_abs", LAST, after="lag2_1")
+        fetch_less("d21_", b1_sb, "neg_x2_", LAST)
+        nc.scalar.activation(out=d21_abs[:], in_=d21[:], func=ACT.Abs, scale=1.0)
+        new("neg_top", LAST)
+        for e in range(2):
+            combine("neg_top", "d21_", 0.0, ALU.min, ALU.add, "neg_x2_", LAST, e)
+        zw, zs = quantise_z(0, z_woven)
+        first_accs = []
+        for s0, b in ((0, 1), (SUB, 2)):
+            acc = bank(b, [P, PACK, SUB], "o_acc")
+            for t in range(PACK):
+                product(acc[:, t, :], t, zw[:, s0 : s0 + SUB], zs[:, s0 : s0 + SUB])
+            first_accs.append(acc)
+
+        new("top_less_x3_", LAST, after="z0")
+        new("gain", LAST)
+        new("neg_md", LAST)
         factors = keep.tile([P, 2, 2, CHUNK], F32, name="factors", tag="turned2_1", align_bytes=64)
-        st["gain_abs", 3], st["sig", 3] = factors[:, 0], factors[:, 1]
+        vals["gain_abs", LAST], vals["sig", LAST] = factors[:, 0], factors[:, 1]
+        fetch_less("top_less_x3_", b3_sb, "neg_top", LAST)
         for e in range(2):
-            fetch_over(3, e)
+            combine("gain", "top_less_x3_", 1.0, ALU.mult, ALU.min, "d21_abs", LAST, e)
+            nc.scalar.activation(out=part("gain_abs", LAST, e), in_=part("gain", LAST, e), func=ACT.Abs)
         for e in range(2):
-            make_gain(3, 1.0, row(e))
-        for e in range(2):
-            sig_direct(3, row(e))
-        res_woven_a = weave_result(0, accs_a, "neg_md3")
-        weigh(2, gs_sb)
-        weigh(3, gs_sb)
-        store_result(0, accs_a, "turned2_1")
-        z_woven_b = weave(nc.vector.tensor_copy, z[1][:, :, 0:SUB], "z_woven256")
-        z_woven_c = weave(nc.vector.tensor_copy, z[1][:, :, SUB:CHUNK], "z_woven384")
-        zq_b = quantise_z(CHUNK, SUB, z_woven_b)
-        zq_c = quantise_z(CHUNK + SUB, SUB, z_woven_c)
-        hand_on(0, CHUNK, res_woven_a, "z_woven256")
-        res_b = last_product(CHUNK, SUB, zq_b, (3, 5), nc.sync)
-        res_c = last_product(CHUNK + SUB, SUB, zq_c, (4, 6), nc.sync)
-        res_woven_b = weave(nc.scalar.copy, res_b[:], "res_woven256")
-        res_woven_c = weave(nc.vector.tensor_copy, res_c[:], "res_woven384")
-        ow = keep.tile([P, CHUNK], U32, name="ow_last", align_bytes=64)
-        for s0, woven in ((0, res_woven_b), (SUB, res_woven_c)):
-            nc.vector.quantize_mx(
-                out=ow[:, s0 : s0 + SUB].bitcast(FP8X4), scales=out_scales[:, CHUNK + s0 : CHUNK + s0 + SUB], in_=woven[:].rearrange("p n t -> p (n t)")
+            combine("neg_md", "gain", 0.0, ALU.max, ALU.add, "neg_top", LAST, e)
+            nc.scalar.activation(out=part("sig", LAST, e), in_=part("neg_md", LAST, e), func=ACT.Sigmoid, scale=-1.0)
+
+        first_woven = keep.tile([P, CHUNK, PACK], BF16, name="res_woven0", tag="neg_md%d" % LAST, align_bytes=64)
+        for i, acc in enumerate(first_accs):
+            nc.scalar.activation(
+                out=first_woven[:, i * SUB : (i + 1) * SUB, :], in_=acc[:].rearrange("p t n -> p n t"), func=ACT.Copy, scale=OUT_SCALE
             )
-        nc.sync.dma_start(out=words_of(out_1)[:, CHUNK:], in_=ow[:].bitcast(I32))
+        weigh(2)
+        weigh(LAST)
+        first_res = keep.tile([P, PACK, CHUNK], F32, name="res0", tag="turned2_1", align_bytes=64)
+        for i, acc in enumerate(first_accs):
+            nc.scalar.activation(out=first_res[:, :, i * SUB : (i + 1) * SUB], in_=acc[:], func=ACT.Copy, scale=OUT_SCALE)
+        nc.sync.dma_start(out=out_rows[:, :, :CHUNK], in_=first_res[:])
+
+        pieces = (CHUNK, CHUNK + SUB)
+        z_pieces = [weave(nc.vector.tensor_copy, z[1][:, :, j0 - CHUNK : j0 - CHUNK + SUB], "z_woven%d" % j0) for j0 in pieces]
+        z_codes = [quantise_z(j0, woven) for j0, woven in zip(pieces, z_pieces)]
+        first_words = keep.tile([P, CHUNK], U32, name="ow0", tag="z_woven%d" % CHUNK, align_bytes=64)
+        quantise(first_words[:], out_scales[:, :CHUNK], first_woven)
+        nc.sync.dma_start(out=words_of(out_1)[:, :CHUNK], in_=first_words[:].bitcast(I32))
+        results = [closing_product(j0, zw, zs, banks) for j0, (zw, zs), banks in zip(pieces, z_codes, ((3, 5), (4, 6)))]
+        res_pieces = [
+            weave(copy, res[:], "res_woven%d" % j0) for j0, res, copy in zip(pieces, results, (nc.scalar.copy, nc.vector.tensor_copy))
+        ]
+        last_words = keep.tile([P, CHUNK], U32, name="ow_last", align_bytes=64)
+        for j0, woven in zip(pieces, res_pieces):
+            quantise(last_words[:, j0 - CHUNK : j0 - CHUNK + SUB], out_scales[:, j0 : j0 + SUB], woven)
+        nc.sync.dma_start(out=words_of(out_1)[:, CHUNK:], in_=last_words[:].bitcast(I32))
+
         for q in range(4):
-            eng = nc.scalar if q % 2 else nc.sync
-            eng.dma_start(out=out_2[0].bitcast(I32)[4 * q : 4 * q + 4, :], in_=out_scales[32 * q : 32 * q + 4, :].bitcast(I32))
+            queue = nc.scalar if q % 2 else nc.sync
+            queue.dma_start(out=out_2[0].bitcast(I32)[4 * q : 4 * q + 4, :], in_=out_scales[32 * q : 32 * q + 4, :].bitcast(I32))

from contextlib import ExitStack

import concourse.mybir as mybir
from concourse.masks import make_identity

F32 = mybir.dt.float32
BF16 = mybir.dt.bfloat16
I32 = mybir.dt.int32
U32 = mybir.dt.uint32
U16 = mybir.dt.uint16
U8 = mybir.dt.uint8
FP8X4 = mybir.dt.float8_e4m3fn_x4
ALU = mybir.AluOpType
ACT = mybir.ActivationFunctionType

P = 128
PACK = 4
GROUP = 16
K, T, S, H, G = 512, 2048, 512, 512, 2048
FLOPS = 2 * K * H * S + 2 * H * H * S
OUT_SCALE = 0.0625
CHUNK = 256
SUB = 128
UNITS = (((0, 1), 0), ((2, 3), 0), ((0, 1), CHUNK), ((2, 3), CHUNK))
LAST = len(UNITS) - 1


def tile_picked_auction2_none_po_kernel(
    tc, x_words, x_scales, w1_words, w1_scales, gs, d_words, d_scales, offs, b_x1, b_x2, b_x3, kq, out_0, out_1, out_2
):
    nc = tc.nc

    def words_of(dram):
        return dram[0].rearrange("p n t -> p (n t)").bitcast(I32)

    with ExitStack() as ctx:
        keep = ctx.enter_context(tc.tile_pool(name="keep", bufs=1))
        psum = ctx.enter_context(tc.psum_pool(name="psum", bufs=1))

        offs_sb = keep.tile([P, S // GROUP], U16, name="offs_sb")
        b1_sb = keep.tile([P, S // GROUP], U16, name="b1_sb")
        b2_sb = keep.tile([P, S // GROUP], U16, name="b2_sb")
        b3_sb = keep.tile([P, S // GROUP], U16, name="b3_sb")
        kq_sb = keep.tile([P, H // GROUP], U16, name="kq_sb")

        xw_win = keep.tile([P, T], U32, name="xw_win", align_bytes=64)
        dw_win = keep.tile([P, G], U32, name="dw_win", align_bytes=64)
        xs_win = keep.tile([P, T], U8, name="xs_win", align_bytes=64)
        ds_win = keep.tile([P, G], U8, name="ds_win", align_bytes=64)
        w1w_raw = keep.tile([P, H], U32, name="w1w_raw", align_bytes=64)
        w1s_raw = keep.tile([P, H], U8, name="w1s_raw", tag="w1s_raw", align_bytes=64)
        w1w = keep.tile([P, H], U32, name="w1w", align_bytes=64)
        w1s = keep.tile([P, H], U8, name="w1s", align_bytes=64)
        xw = keep.tile([P, S], U32, name="xw", align_bytes=64)
        xs = keep.tile([P, S], U8, name="xs", align_bytes=64)
        ds_pick = keep.tile([P, H], U8, name="ds_pick", align_bytes=64)
        ds = keep.tile([P, H], U8, name="ds", align_bytes=64)
        out_scales = keep.tile([P, S], U8, name="out_scales", align_bytes=64)
        gs_sb = keep.tile([P, PACK], F32, name="gs_sb")

        def deal(dst, src):
            nc.vector.tensor_copy(out=dst.rearrange("p (t m) -> p m t", t=PACK), in_=src.rearrange("p (m t) -> p m t", t=PACK))

        def bank(i, shape, name):
            return psum.tile(shape, F32, name=name, tag="bank%d" % i)

        nc.vector.memset(ds_win[:].bitcast(I32), 0)
        for scale_tile in (xs_win, w1s_raw, ds):
            nc.gpsimd.memset(scale_tile[:].bitcast(I32), 0)
        ident = keep.tile([P, P], F32, name="ident", align_bytes=64)
        make_identity(nc, ident[:])

        nc.sync.dma_start(offs_sb[:], offs)
        nc.sync.dma_start(kq_sb[:], kq)
        for r in range(4):
            nc.sync.dma_start(out=xs_win[r:P:32, :].bitcast(I32), in_=x_scales[0].bitcast(I32)[r:16:4, :])
        nc.sync.dma_start(out=ds_win[0:P:8, :].bitcast(I32), in_=d_scales[0].bitcast(I32))
        nc.sync.dma_start(out=xw_win[:].bitcast(I32), in_=words_of(x_words))
        nc.sync.dma_start(out=w1w_raw[:].bitcast(I32), in_=words_of(w1_words))
        for r in range(4):
            nc.sync.dma_start(out=w1s_raw[r:P:32, :].bitcast(I32), in_=w1_scales[0].bitcast(I32)[r:16:4, :])
        nc.sync.dma_start(out=dw_win[:].bitcast(I32), in_=words_of(d_words))
        nc.sync.dma_start(b2_sb[:], b_x2)
        nc.sync.dma_start(b1_sb[:], b_x1)
        nc.sync.dma_start(b3_sb[:], b_x3)
        nc.sync.dma_start(out=gs_sb[:], in_=gs.rearrange("(p t) o -> p (t o)", t=PACK))

        half = S // 2
        w1_moves = ((w1w[:].bitcast(I32), w1w_raw[:].bitcast(I32)), (w1s[:], w1s_raw[:]))
        nc.vector.tensor_copy(out=xs[:], in_=xs_win[:].indirect(offs_sb[:]))
        nc.vector.tensor_copy(out=ds_pick[:], in_=ds_win[:].indirect(kq_sb[:]))
        for j0 in (0, half):
            entries = offs_sb[:, j0 // GROUP : (j0 + half) // GROUP]
            nc.vector.tensor_copy(out=xw[:, j0 : j0 + half], in_=xw_win[:].indirect(entries))
        for dst, src in w1_moves:
            nc.vector.tensor_copy(out=dst[:, :P], in_=src.rearrange("p (m t) -> p m t", t=PACK)[:, :, 0])
        for dst, src in w1_moves:
            nc.vector.tensor_copy(
                out=dst[:, P:].rearrange("p (t m) -> p m t", t=PACK - 1), in_=src.rearrange("p (m t) -> p m t", t=PACK)[:, :, 1:]
            )
        ds_dealt = keep.tile([P, H], U8, name="ds_dealt", tag="w1s_raw", align_bytes=64)
        deal(ds_dealt[:], ds_pick[:])
        for r in range(4):
            nc.sync.dma_start(out=ds[r:P:32, :].bitcast(I32), in_=ds_dealt[8 * r : P : 32, :].bitcast(I32))

        neg_y = [keep.tile([P, S], F32, name="neg_y%d" % t) for t in range(PACK)]
        for b, (t, j0, n) in enumerate(((0, 0, half), (0, half, half), (1, 0, S), (2, 0, S), (3, 0, S))):
            acc = bank(b, [P, n], "y_acc")
            nc.tensor.matmul_mx(
                out=acc[:],
                lhsT=w1w[:, t * P : (t + 1) * P].bitcast(FP8X4),
                lhsT_scale=w1s[:, t * P : (t + 1) * P],
                rhs=xw[:, j0 : j0 + n].bitcast(FP8X4),
                rhs_scale=xs[:, j0 : j0 + n],
                start=True,
                stop=True,
            )
            nc.scalar.activation(out=neg_y[t][:, j0 : j0 + n], in_=acc[:], func=ACT.Copy, scale=-1.0)

        vals = {}
        z = [keep.tile([P, PACK, CHUNK], BF16, name="z%d" % c, tag="z%d" % c, align_bytes=64) for c in range(S // CHUNK)]
        out_rows = out_0.rearrange("(p t) j -> p t j", t=PACK)

        def new(name, u, after=None):
            vals[name, u] = keep.tile([P, 2, CHUNK], F32, name="%s%d" % (name, u), tag=after or "%s%d" % (name, u), align_bytes=64)
            return vals[name, u]

        def new_rows(name, u, after=None):
            vals[name, u] = [
                keep.tile([P, CHUNK], F32, name="%s%d_%d" % (name, u, e), tag="%s_%d" % (after or "%s%d" % (name, u), e), align_bytes=64)
                for e in range(2)
            ]

        def part(name, u, e):
            held = vals[name, u]
            return held[e][:] if isinstance(held, list) else held[:, e, :]

        def picked(lst, u, e):
            ts, j0 = UNITS[u]
            return neg_y[ts[e]][:].indirect(lst[:, j0 // GROUP : (j0 + CHUNK) // GROUP])

        def fetch_neg_x2(u, after=None):
            new_rows("neg_x2_", u, after)
            for e in range(2):
                nc.vector.tensor_copy(out=part("neg_x2_", u, e), in_=picked(b2_sb, u, e))

        def fetch_less(name, lst, base, u):
            for e in range(2):
                nc.vector.tensor_tensor(out=part(name, u, e), in0=picked(lst, u, e), in1=part(base, u, e), op=ALU.subtract)

        def combine(name, in0, scalar, op0, op1, in1, u, e):
            nc.vector.scalar_tensor_tensor(out=part(name, u, e), in0=part(in0, u, e), scalar=scalar, in1=part(in1, u, e), op0=op0, op1=op1)

        def turn(dst, *terms):
            for c0 in range(0, CHUNK, P):
                for i, term in enumerate(terms):
                    nc.tensor.matmul(
                        out=dst[:, c0 : c0 + P], lhsT=term[:, c0 : c0 + P], rhs=ident[:], is_transpose=True, start=i == 0, stop=i == len(terms) - 1
                    )

        def order_bids(u, x2_after=None, lead_after=None):
            fetch_neg_x2(u, x2_after)
            d21 = new("d21_", u)
            new_rows("d23_", u)
            fetch_less("d21_", b1_sb, "neg_x2_", u)
            nc.scalar.activation(out=new("lead", u, lead_after)[:], in_=d21[:], func=ACT.Relu, scale=-1.0)
            fetch_less("d23_", b3_sb, "neg_x2_", u)
            new_rows("lag", u)
            for e in range(2):
                combine("lag", "d21_", 0.0, ALU.max, ALU.min, "d23_", u, e)

        def factors_by_transposes(u, banks):
            turned = [keep.tile([P, 3, CHUNK], F32, name="turned%d_%d" % (u, e), tag="turned%d_%d" % (u, e), align_bytes=64) for e in range(2)]
            for e in range(2):
                sums = bank(banks[e], [P, 2, CHUNK], "sums")
                gain, neg_rival = sums[:, 0, :], sums[:, 1, :]
                turn(neg_rival, part("neg_x2_", u, e), part("lag", u, e))
                turn(gain, part("lead", u, e), part("lag", u, e))
                nc.scalar.activation(out=turned[e][:, 0, :], in_=gain, func=ACT.Relu, scale=-1.0)
                nc.scalar.activation(out=turned[e][:, 1, :], in_=neg_rival, func=ACT.Copy)
                nc.scalar.activation(out=turned[e][:, 2, :], in_=gain, func=ACT.Abs)
            new_rows("sig", u)
            neg_md, vals["gain_abs", u] = bank(banks[2], [P, 2, CHUNK], "neg_md"), bank(banks[3], [P, 2, CHUNK], "gain_abs")
            for e in range(2):
                turn(neg_md[:, e, :], turned[e][:, 0, :], turned[e][:, 1, :])
                turn(part("gain_abs", u, e), turned[e][:, 2, :])
            for e in range(2):
                nc.scalar.activation(out=part("sig", u, e), in_=neg_md[:, e, :], func=ACT.Sigmoid, scale=-1.0)

        def weigh(u):
            ts, j0 = UNITS[u]
            for e, t in enumerate(ts):
                nc.vector.scalar_tensor_tensor(
                    out=z[j0 // CHUNK][:, t, :], in0=part("gain_abs", u, e), scalar=gs_sb[:, t : t + 1], in1=part("sig", u, e),
                    op0=ALU.mult, op1=ALU.mult,
                )

        def weave(copy, src, name, after=None):
            woven = keep.tile([P, src.shape[2], PACK], BF16, name=name, tag=after or name, align_bytes=64)
            copy(out=woven[:], in_=src.rearrange("p t n -> p n t"))
            return woven

        def quantise(words, scales, woven):
            nc.vector.quantize_mx(out=words.bitcast(FP8X4), scales=scales, in_=woven[:].rearrange("p n t -> p (n t)"))

        def quantise_z(j0, woven):
            zw = keep.tile([P, woven[:].shape[1]], U32, name="zw%d" % j0, align_bytes=64)
            zs = keep.tile([P, woven[:].shape[1]], U8, name="zs%d" % j0, align_bytes=64)
            quantise(zw[:], zs[:], woven)
            return zw, zs

        def product(out, t, zw, zs):
            nc.tensor.matmul_mx(
                out=out,
                lhsT=dw[:, t * P : (t + 1) * P].bitcast(FP8X4),
                lhsT_scale=ds[:, t * P : (t + 1) * P],
                rhs=zw.bitcast(FP8X4),
                rhs_scale=zs,
                start=True,
                stop=True,
            )

        def closing_product(j0, zw, zs, banks):
            res = keep.tile([P, PACK, SUB], F32, name="res%d" % j0, align_bytes=64)
            for i, b in enumerate(banks):
                acc = bank(b, [P, 2, SUB], "o_acc")
                for e in range(2):
                    product(acc[:, e, :], 2 * i + e, zw[:], zs[:])
                if i == 0:
                    nc.scalar.activation(out=res[:, 0:2, :], in_=acc[:], func=ACT.Copy, scale=OUT_SCALE)
                else:
                    nc.vector.tensor_scalar(out=res[:, 2:4, :], in0=acc[:], scalar1=OUT_SCALE, scalar2=0.0, op0=ALU.mult, op1=ALU.add)
            nc.sync.dma_start(out=out_rows[:, :, j0 : j0 + SUB], in_=res[:])
            return res

        dw_pick = keep.tile([P, H], U32, name="dw_pick", align_bytes=64)
        nc.vector.tensor_copy(out=dw_pick[:], in_=dw_win[:].indirect(kq_sb[:]))

        order_bids(0)
        factors_by_transposes(0, (5, 6, 7, 0))
        order_bids(1, x2_after="d23_0", lead_after="turned0_0")
        factors_by_transposes(1, (5, 6, 3, 4))
        order_bids(2, x2_after="d23_1", lead_after="turned1_0")
        weigh(0)
        weigh(1)
        dw = keep.tile([P, H], U32, name="dw", tag="sig1_0", align_bytes=64)
        deal(dw[:].bitcast(I32), dw_pick[:].bitcast(I32))
        factors_by_transposes(2, (5, 6, 7, 0))

        z_woven = weave(nc.scalar.copy, z[0][:], "z_woven0", after="lag2_0")
        fetch_neg_x2(LAST, after="sig0")
        d21, d21_abs = new("d21_", LAST, after="sig1_1"), new("d21_abs", LAST, after="lag2_1")
        fetch_less("d21_", b1_sb, "neg_x2_", LAST)
        nc.scalar.activation(out=d21_abs[:], in_=d21[:], func=ACT.Abs, scale=1.0)
        new("neg_top", LAST)
        for e in range(2):
            combine("neg_top", "d21_", 0.0, ALU.min, ALU.add, "neg_x2_", LAST, e)
        zw, zs = quantise_z(0, z_woven)
        first_accs = []
        for s0, b in ((0, 1), (SUB, 2)):
            acc = bank(b, [P, PACK, SUB], "o_acc")
            for t in range(PACK):
                product(acc[:, t, :], t, zw[:, s0 : s0 + SUB], zs[:, s0 : s0 + SUB])
            first_accs.append(acc)

        new("top_less_x3_", LAST, after="z0")
        new("gain", LAST)
        new("neg_md", LAST)
        factors = keep.tile([P, 2, 2, CHUNK], F32, name="factors", tag="turned2_1", align_bytes=64)
        vals["gain_abs", LAST], vals["sig", LAST] = factors[:, 0], factors[:, 1]
        fetch_less("top_less_x3_", b3_sb, "neg_top", LAST)
        for e in range(2):
            combine("gain", "top_less_x3_", 1.0, ALU.mult, ALU.min, "d21_abs", LAST, e)
            nc.scalar.activation(out=part("gain_abs", LAST, e), in_=part("gain", LAST, e), func=ACT.Abs)
        for e in range(2):
            combine("neg_md", "gain", 0.0, ALU.max, ALU.add, "neg_top", LAST, e)
            nc.scalar.activation(out=part("sig", LAST, e), in_=part("neg_md", LAST, e), func=ACT.Sigmoid, scale=-1.0)

        first_woven = keep.tile([P, CHUNK, PACK], BF16, name="res_woven0", tag="neg_md%d" % LAST, align_bytes=64)
        for i, acc in enumerate(first_accs):
            nc.scalar.activation(
                out=first_woven[:, i * SUB : (i + 1) * SUB, :], in_=acc[:].rearrange("p t n -> p n t"), func=ACT.Copy, scale=OUT_SCALE
            )
        weigh(2)
        weigh(LAST)
        first_res = keep.tile([P, PACK, CHUNK], F32, name="res0", tag="turned2_1", align_bytes=64)
        for i, acc in enumerate(first_accs):
            nc.scalar.activation(out=first_res[:, :, i * SUB : (i + 1) * SUB], in_=acc[:], func=ACT.Copy, scale=OUT_SCALE)
        nc.sync.dma_start(out=out_rows[:, :, :CHUNK], in_=first_res[:])

        pieces = (CHUNK, CHUNK + SUB)
        z_pieces = [weave(nc.vector.tensor_copy, z[1][:, :, j0 - CHUNK : j0 - CHUNK + SUB], "z_woven%d" % j0) for j0 in pieces]
        z_codes = [quantise_z(j0, woven) for j0, woven in zip(pieces, z_pieces)]
        first_words = keep.tile([P, CHUNK], U32, name="ow0", tag="z_woven%d" % CHUNK, align_bytes=64)
        quantise(first_words[:], out_scales[:, :CHUNK], first_woven)
        nc.sync.dma_start(out=words_of(out_1)[:, :CHUNK], in_=first_words[:].bitcast(I32))
        results = [closing_product(j0, zw, zs, banks) for j0, (zw, zs), banks in zip(pieces, z_codes, ((3, 5), (4, 6)))]
        res_pieces = [
            weave(copy, res[:], "res_woven%d" % j0) for j0, res, copy in zip(pieces, results, (nc.scalar.copy, nc.vector.tensor_copy))
        ]
        last_words = keep.tile([P, CHUNK], U32, name="ow_last", align_bytes=64)
        for j0, woven in zip(pieces, res_pieces):
            quantise(last_words[:, j0 - CHUNK : j0 - CHUNK + SUB], out_scales[:, j0 : j0 + SUB], woven)
        nc.sync.dma_start(out=words_of(out_1)[:, CHUNK:], in_=last_words[:].bitcast(I32))

        for q in range(4):
            queue = nc.scalar if q % 2 else nc.sync
            queue.dma_start(out=out_2[0].bitcast(I32)[4 * q : 4 * q + 4, :], in_=out_scales[32 * q : 32 * q + 4, :].bitcast(I32))
